import numpy as np, ml_dtypes
CORES = [1,5,17,21,33,37,49,53]
N = 8
BF = ml_dtypes.bfloat16
def f(rng, *shape):
    return (rng.standard_normal(shape, dtype=np.float32) * np.exp2(rng.integers(-2, 3, shape[:-1] + (1,)))).astype(BF)
def wide(rng, *shape):
    v = f(rng, *shape).astype(np.float32); k = shape[:-2] + (1, shape[-1])
    return (v * np.exp2(rng.integers(-6, 7, k)) * (rng.random(k) > 0.0625)).astype(BF)
def gentries(a):
    return np.ascontiguousarray(a.reshape(8, 16, -1).transpose(0, 2, 1)).reshape(8, -1)
def gtable(e):
    e = np.asarray(e); return np.ascontiguousarray(e.reshape(8, -1, 16).transpose(0, 2, 1)).reshape(128, -1).astype(np.int32)
S, SH, TL, E, CAP = 4096, 16, 32, 64, 320
D = 256 * SH
def scene(rng):
    v = rng.random((N, 16, D)) ** 2; u = rng.random((N, 16, D)); v = np.where(u < 0.0625, 0.0, np.where(u > 0.96875, 1.0, v))
    o = rng.random((N, 8, S)) ** 2; u = rng.random((N, 8, S)); o = np.where(u < 0.03125, 0.0, np.where(u > 0.9375, 1.0, o))
    m = np.stack([rng.integers(0, SH, (N, 8, S)), rng.integers(0, 8, (N, 8, S)), rng.integers(0, 8, (N, 8, S))], 2).reshape(N, 24, S)
    return {"dic": v.astype(np.float32).astype(BF), "opa": o.astype(np.float32).astype(BF), "hue": f(rng, N, 24, S), "geo": m.astype(np.int32)}
def owners(rng, bias):
    key = rng.random((N, 8, N * CAP)) + np.repeat(bias, CAP, -1)
    w = np.argsort(key, -1)[:, :, :TL * E] // CAP
    return np.take_along_axis(w, np.argsort(rng.random(w.shape), -1), -1)
def lists(w, s, gone):
    e = np.where(gone, -1, w * S + s); return np.stack([gtable(e[r]) for r in range(N)])
def setup_inputs(rng):
    d = scene(rng); w = owners(rng, np.zeros((N, 8, N)))
    d["ent"] = lists(w, rng.integers(0, S, w.shape), rng.random(w.shape) < 0.1); return d
def setup_inputs_full(rng):
    d = scene(rng); r = np.arange(N)[:, None]; g = np.arange(8)[None, :]; bias = np.zeros((N, 8, N))
    bias[r, g, (r + 1 + g % (N - 1)) % N] = -1; bias[r, g[:, 4:], r] = -1
    w = owners(rng, bias); w[:, 1::2] = np.sort(w[:, 1::2], -1)
    whole = np.take_along_axis(bias, w, -1) < 0
    d["ent"] = lists(w, rng.integers(0, S, w.shape), (rng.random(w.shape) < 0.1) & ~whole); return d
def setup_inputs_ends(rng):
    d = scene(rng); b = rng.integers(0, 2, (N, 8, 3, S)) * np.array([SH - 1, 7, 7])[:, None]; d["geo"] = b.reshape(N, 24, S).astype(np.int32)
    r = np.arange(N)[:, None, None, None]; g = np.arange(8)[:, None, None]; t = np.arange(TL)[:, None]; j = np.arange(E)
    w = owners(rng, np.zeros((N, 8, N))).reshape(N, 8, TL, E)
    s = np.where(rng.random((N, 8, TL, 1)) < 0.5, rng.integers(0, 2, (N, 8, TL, E)) * (S - 1), rng.integers(0, S, (N, 8, TL, 1)))
    kind = (r + g + t) % 8
    gone = (kind == 0) | ((kind == 1) & (j > 0)) | ((kind == 2) & (j < E - 1)) | ((kind > 2) & ((rng.random((N, 8, TL, E)) < 0.1) | (w == (r + 1 + g % (N - 1)) % N)))
    gone = gone | ((w == (r + 1 + g % (N - 1)) % N) & (kind < 3))
    gone = gone | (g == r % 8) | ((g == (r + 3) % 8) & (w != (r + 1 + (g + 1) % (N - 1)) % N))
    d["ent"] = lists(w.reshape(N, 8, -1), s.reshape(N, 8, -1), gone.reshape(N, 8, -1)); return d
def setup_inputs_solid(rng):
    d = setup_inputs(rng); u = rng.random((N, 16, D))
    d["dic"] = np.where(u < 0.125, 0.0, np.where(u < 0.25, 1.0, d["dic"].astype(np.float32))).astype(np.float32).astype(BF)
    d["opa"] = np.where(rng.random((N, 8, S)) < 0.5, 1.0, d["opa"].astype(np.float32)).astype(np.float32).astype(BF); return d
def setup_inputs_spread(rng):
    d = scene(rng); d["hue"] = wide(rng, N, 24, S); w = owners(rng, rng.random((N, 8, N)))
    d["ent"] = lists(w, rng.integers(0, S, w.shape), rng.random(w.shape) < 0.1); return d
def check_inputs(d):
    bad = []
    for a in ("dic", "opa"):
        v = d[a].astype(np.float32)
        if not ((v >= 0) & (v <= 1)).all(): bad.append(a + " from 0 to 1")
    if not np.isfinite(d["hue"].astype(np.float32)).all(): bad.append("hue finite")
    m = d["geo"].reshape(N, 8, 3, S)
    if not ((m >= 0).all() and (m[:, :, 0] < SH).all() and (m[:, :, 1:] < 8).all()): bad.append("geo in range")
    e = np.stack([gentries(d["ent"][r]) for r in range(N)])
    if not ((e >= -1) & (e < N * S)).all(): bad.append("ent in range")
    if any((np.sum((e >= q * S) & (e < q * S + S), -1) > CAP).any() for q in range(N)): bad.append("at most CAP entries")
    return bad
def reference(dic, opa, hue, geo, ent):
    y = np.zeros((N, 128, 3 * TL), np.float64); F, O, H = dic.astype(np.float64), opa.astype(np.float64), hue.astype(np.float64)
    g = np.arange(8)[:, None]; t = np.arange(TL * E) // E; tx, ty = t & 7, t >> 3
    for r in range(N):
        e = gentries(ent[r]); k = np.maximum(e, 0).astype(np.int64); q = k // S; s = k - q * S
        at = 256 * geo[q, 3 * g, s] + 16 * (ty - geo[q, 3 * g + 2, s] + 8) + (tx - geo[q, 3 * g + 1, s] + 8)
        a = F[q, :, at] * (O[q, g, s] * (e >= 0))[:, :, None]
        a = a.reshape(8, TL, E, 16); left = np.multiply.accumulate(1 - a, axis=2)
        w = a * np.concatenate([np.ones((8, TL, 1, 16)), left[:, :, :-1]], 2)
        c = H[q[:, :, None], 3 * g[:, :, None] + np.arange(3), s[:, :, None]].reshape(8, TL, E, 3)
        y[r] = np.einsum("gtep,gtec->gpct", w, c).reshape(128, 3 * TL)
    return {"y": y.astype(np.float32)}

@@ -1,0 +1,414 @@
+from concourse.bass import DstId, RemoteDMATransfer
+from concourse.mybir import AluOpType as OP, ActivationFunctionType as AF
+
+N, S, CAP, NE = 8, 4096, 320, 2048
+LW = CAP // 16
+Z = 16
+SP = NE + 128
+BIG = 8192.0
+DUMP = 8192 - 1280 + 1 - SP
+UW = 132
+
+SCRATCH = {
+    "ent_s": ("sbuf", [128, 128], "int32"),
+    "i1": ("sbuf", [128, 160], "int32"), "i1s": ("sbuf", [128, 160], "int32"), "e0": ("sbuf", [128, 160], "bfloat16"),
+    "i2": ("sbuf", [128, 16], "int32"), "i2s": ("sbuf", [128, 16], "int32"), "dl": ("sbuf", [128, 16], "float32"),
+    "i3": ("sbuf", [128, 128], "int32"), "i3s": ("sbuf", [128, 128], "int32"),
+    "bd": ("sbuf", [128, 128], "bfloat16"), "nbd": ("sbuf", [128, 128], "bfloat16"),
+    "l0": ("sbuf", [128, 128], "bfloat16"), "l1": ("sbuf", [128, 128], "bfloat16"),
+    "offc": ("sbuf", [128, 128], "bfloat16"), "d0": ("sbuf", [128, 1024], "float32"),
+    "one": ("sbuf", [128, 128], "bfloat16"), "onef": ("sbuf", [128, 128], "float32"),
+    "idf": ("sbuf", [128, 128], "float32"), "selc": ("sbuf", [128, 24], "bfloat16"),
+    "kc": ("sbuf", [128, 8], "int32"), "kf": ("sbuf", [128, 8], "float32"), "wc": ("sbuf", [128, 8], "float32"),
+    "ip": ("sbuf", [128, 8], "int32"), "pick": ("sbuf", [128, 8], "uint16"),
+    "um": ("sbuf", [128, 16 * UW], "bfloat16"),
+    "rw": ("sbuf", [128, 160], "bfloat16"), "rb": ("sbuf", [128, 160], "bfloat16"), "bo": ("sbuf", [128, 128], "bfloat16"),
+    "ob": ("sbuf", [128, 128], "bfloat16"), "hi": ("sbuf", [128, 128], "bfloat16"), "lo": ("sbuf", [128, 128], "bfloat16"),
+    "mk": ("sbuf", [128, 1024], "bfloat16"), "sc": ("sbuf", [128, 1024], "bfloat16"), "ms": ("sbuf", [128, 1024], "float32"),
+    "slot": ("sbuf", [128, 128], "uint16"), "fin": ("sbuf", [128, 128], "uint16"),
+    "vv": ("sbuf", [128, NE], "bfloat16"), "wn": ("sbuf", [128, SP + N * CAP], "bfloat16"),
+    "rqo": ("sbuf", [128, N * LW], "int32"), "rqi": ("sbuf", [128, N * LW], "int32"),
+    "su": ("sbuf", [128, N * LW], "uint16"), "of": ("sbuf", [128, N * LW], "int32"),
+    "cf": ("sbuf", [128, N * LW], "float32"), "cu": ("sbuf", [128, N * LW], "uint16"),
+    "dw": ("sbuf", [128, S], "bfloat16"), "aw": ("sbuf", [128, S], "bfloat16"),
+    "gi": ("sbuf", [128, 768], "int32"), "gb": ("sbuf", [128, 768], "bfloat16"),
+    "gq": ("sbuf", [128, N * CAP], "bfloat16"), "fq": ("sbuf", [128, N * CAP], "bfloat16"),
+    "gw": ("sbuf", [128, Z + N * CAP], "bfloat16"), "fw": ("sbuf", [128, N * CAP], "bfloat16"),
+    "gout": ("dram", [6, 128, CAP // 4], "bfloat16"), "gin": ("dram", [6, 128, CAP // 4], "bfloat16"),
+    "ge": ("sbuf", [128, NE], "bfloat16"), "al": ("sbuf", [128, Z + N * CAP], "float32"),
+    "ct": ("sbuf", [128, 768], "float32"), "st": ("sbuf", [128, 256], "bfloat16"),
+    "om": ("sbuf", [128, NE + 4], "float32"), "li": ("sbuf", [128, NE], "float32"),
+    "ww": ("sbuf", [128, NE], "float32"), "wt": ("sbuf", [128, NE], "float32"),
+    "ya": ("sbuf", [128, 768], "float32"), "yo": ("sbuf", [128, 96], "float32"),
+}
+for _b in range(8):
+    SCRATCH["p%d" % _b] = ("psum", [128, 512], "float32")
+
+SEMAPHORES = ["cv", "ca", "ct", "cg", "d_ent", "d_geo", "d_dic", "d_att", "d_pk", "d_un", "d_y",
+              "sent", "rq0", "rq1", "rq2", "rq3", "g_far", "g_near", "f0", "f1", "f2", "f3"]
+
+
+def orders(T, topo, rank):
+    chips = sorted(set(topo.chip(c) for c in T.cores))
+    on = [[r for r in range(N) if topo.chip(T.cores[r]) == ch] for ch in chips]
+    a = chips.index(topo.chip(T.cores[rank]))
+    tail = [r for r in on[a] if r != rank] + [rank]
+    ask = [r for k in range(1, len(chips)) for r in on[(a - k) % len(chips)]] + tail
+    serve = [r for k in range(1, len(chips)) for r in on[(a + k) % len(chips)]] + tail
+    return ask, serve
+
+
+def rank_program(g, core, T, topo):
+    rank = T.rank_of(core)
+    if rank is None:
+        return
+    ask, serve = orders(T, topo, rank)
+    Q = {"v": g.vector, "a": g.scalar, "t": g.tensor, "g": g, "s": g.sync}
+    own = {"v": "cv", "a": "ca", "t": "ct", "g": "cg"}
+    count, seen = {}, {}
+
+    def wait(q, deps):
+        need = {}
+        for d in deps:
+            if d is not None and d[1] > need.get(d[0], 0):
+                need[d[0]] = d[1]
+        for s, v in need.items():
+            if seen.get((q, s), 0) < v:
+                Q[q].wait_ge(T.sem[s], v)
+                seen[(q, s)] = v
+
+    def op(q, deps, make, mark=True):
+        wait(q, deps)
+        ins = make(Q[q])
+        if not mark:
+            return None
+        s = own[q]
+        count[s] = count.get(s, 0) + 1
+        ins.then_inc(T.sem[s], 1)
+        return (s, count[s])
+
+    def dma(s, deps, out, in_):
+        wait("s", deps)
+        g.sync.dma_start(out, in_).then_inc(T.sem[s], 16)
+        count[s] = count.get(s, 0) + 16
+        return (s, count[s])
+
+    def ts(deps, out, in0, s1, o0, s2=None, o1=None):
+        if o1 is None:
+            return op("v", deps, lambda e: e.tensor_scalar(out, in0, s1, None, o0))
+        return op("v", deps, lambda e: e.tensor_scalar(out, in0, s1, s2, o0, o1))
+
+    def tt(deps, out, a, b, o):
+        return op("v", deps, lambda e: e.tensor_tensor(out, a, b, o))
+
+    def cp(deps, out, a):
+        return op("v", deps, lambda e: e.tensor_copy(out, a))
+
+    def fill(deps, out, c):
+        return op("v", deps, lambda e: e.memset(out, c))
+
+    def act(deps, out, a, **kw):
+        f = AF.Identity if kw else AF.Copy
+        return op("a", deps, lambda e: e.activation(out, a, f, **kw))
+
+    def mm(deps, out, lhsT, rhs, start, stop, mark=None):
+        return op("t", deps, lambda e: e.matmul(out, lhsT, rhs, start, stop), stop if mark is None else mark)
+
+    def iota(out, pattern, base, cm, small=False):
+        if small:
+            return op("g", [], lambda e: e.iota(out, pattern, base, cm, allow_small_or_imprecise_dtypes=True))
+        return op("g", [], lambda e: e.iota(out, pattern, base, cm))
+
+    def cols(i, w, at=0):
+        return slice(at + w * i, at + w * i + w)
+
+    def bits(engs):
+        m = 0
+        for e in engs:
+            m |= 1 << e
+        return m
+
+    def send(deps, items):
+        wait("g", deps)
+        trs = []
+        for r, engs, s, src, dst in items:
+            rid, pid, _ = topo.addr(T.cores[r])
+            trs.append(RemoteDMATransfer(dst_ids=[DstId(rid=rid, pnc=pid)], dma_engine_mask=bits(engs),
+                                         remote_sem=T.sem[s], src=src, dst=dst))
+            count["sent"] = count.get("sent", 0) + len(engs)
+        g.remote_dma_fused(trs, local_sem=T.sem["sent"])
+
+    far = topo.engines(core, T.cores[ask[0]])
+    near = [e for e in topo.engines(core, T.cores[ask[6]]) if e not in far]
+    hf, hn = len(far) // 2, len(near) // 2
+    P = [T["p%d" % b] for b in range(8)]
+
+    ent = dma("d_ent", [], T.ent_s[:], T.ent[:])
+    for a in range(3):
+        geo = dma("d_geo", [], T.gi[:, cols(a, 256)], T.geo[a:24:3, :])
+    for k in range(8):
+        dic = dma("d_dic", [], T.dw[cols(k, 16), :], T.dic[:])
+
+    i1 = iota(T.i1[:], [[-16, 10], [256, 16]], 16, 1)
+    i2 = iota(T.i2[:], [[-1, 16]], 16, 1)
+    i3 = iota(T.i3[:], [[-16, 8], [0, 16]], 0, 1)
+    offc = iota(T.offc[:], [[16, 4], [1, 8], [0, 4]], 0, 0, True)
+    one = fill([], T.one[:], 1.0)
+    onef = fill([], T.onef[:], 1.0)
+    x1 = ts([i1], T.i1s[:], T.i1[:], 4, OP.arith_shift_right)
+    x2 = ts([i2], T.i2s[:], T.i2[:], 15, OP.bitwise_and)
+    e0 = ts([x1], T.e0[:], T.i1s[:], 0.0, OP.is_equal)
+    dl = ts([x2], T.dl[:], T.i2s[:], 0.0, OP.is_equal)
+    x3 = ts([i3], T.i3s[:], T.i3[:], 4, OP.arith_shift_right)
+    um = [None] * 16
+    um[0] = ts([e0, dl], T.um[:, 0:UW], T.e0[:, 14:14 + UW], T.dl[:, 0:1], OP.mult)
+    nbd = ts([x3], T.nbd[:], T.i3s[:], 0.0, OP.is_equal, -1.0, OP.mult)
+    bd = ts([x3], T.bd[:], T.i3s[:], 0.0, OP.is_equal)
+    for p in (4, 8, 12):
+        um[p] = ts([e0, dl], T.um[:, cols(p, UW)], T.e0[:, 14:14 + UW], T.dl[:, p:p + 1], OP.mult)
+    for b in range(1, 4):
+        for p in range(b, 16, 4):
+            um[p] = act([e0, dl], T.um[:, cols(p, UW)], T.e0[:, 14:14 + UW], scale=T.dl[:, p:p + 1])
+    l0 = op("g", [nbd], lambda e: e.affine_select(T.l0[:], T.nbd[:], [[-1, 128]], OP.is_gt, 0.0, 0, 1))
+    l1 = op("g", [l0], lambda e: e.affine_select(T.l1[:], T.l0[:], [[-1, 128]], OP.not_equal, BIG, 0, 1))
+    d0 = iota(T.d0[:], [[-16, 128], [8192, 8]], DUMP + 16 * 127, 1, True)
+    kc = iota(T.kc[:, 0:1], [[0, 1]], 0, 1)
+    ip = iota(T.ip[:, 0:6], [[2, 3], [384, 2]], 0, 0)
+    awz = iota(T.aw[:, 0:NE], [[0, NE]], 0, 0, True)
+
+    magic = 1.5 * 2.0 ** 31
+    hi = ts([ent], T.hi[:], T.ent_s[:], magic, OP.add, magic, OP.subtract)
+    ob = ts([ent], T.ob[:], T.ent_s[:], 2.0 ** -12, OP.mult, 135.5 + 2.0 ** -13, OP.add)
+    lo = tt([hi], T.lo[:], T.ent_s[:], T.hi[:], OP.subtract)
+    mks = [ts([ob], T.mk[:, i:1024:8], T.ob[:], 136.0 + ask[i], OP.is_equal) for i in range(N)]
+    scs = [op("v", [mks[i], one], lambda e, i=i: e.tensor_tensor_scan(
+        T.sc[:, i:1024:8], T.one[:], T.mk[:, i:1024:8], 20.0 * (i - 4), OP.mult, OP.add)) for i in range(N)]
+    wnz = fill([], T.wn[:, SP:SP + N * CAP], 0.0)
+
+    unw = [None] * 4
+    cnt = [None, None]
+
+    def unwrap(b):
+        for j in range(4):
+            o = P[b][:, j:512:4]
+            u = UW * (b + 4 * j)
+            mm([um[b + 4 * j], offc], o, T.um[:, u:u + 128], T.offc[:], True, False)
+            mm([hi], o, T.um[:, u + 2:u + 130], T.hi[:], False, False)
+            unw[b] = mm([lo], o, T.um[:, u + 1:u + 129], T.lo[:], False, True, j == 3)
+
+    unwrap(0)
+    unwrap(1)
+    for h in range(2):
+        mm([mks[-1], l1], P[4 + h][:], T.l1[:], T.mk[:, cols(h, 512)], True, False)
+    unwrap(2)
+    for h in range(2):
+        cnt[h] = mm([scs[-1], bd], P[4 + h][:], T.bd[:], T.sc[:, cols(h, 512)], False, True)
+    unwrap(3)
+    for b in range(4):
+        vv = act([unw[b]], T.vv[:, b:NE:4], P[b][:])
+
+    for h in range(2):
+        ms = op("v", [cnt[h], d0], lambda e, h=h: e.tensor_tensor_scan(
+            T.ms[:, cols(h, 512)], T.d0[:, cols(h, 512)], P[4 + h][:], 65536.0, OP.min, OP.max))
+    slot = ts([ms], T.slot[:], T.ms[:, 7:1024:8], float(DUMP), OP.subtract)
+    sct = cp([slot, vv, wnz], T.wn[:].indirect(T.slot[:]), T.vv[:])
+
+    w0 = act([dl], T.wc[:, 0:1], T.dl[:, 0:1], scale=64.0, bias=T.dl[:, 2:3])
+    w2 = act([dl], T.wc[:, 2:3], T.dl[:, 2:3], scale=-1.0)
+    w1 = act([w0], T.wc[:, 1:2], T.dl[:, 1:2], scale=64.0, bias=T.wc[:, 0:1])
+    w3 = act([w2], T.wc[:, 3:4], T.dl[:, 1:2], scale=256.0, bias=T.wc[:, 2:3])
+    rw = act([w1], T.rw[:], T.e0[:], scale=T.wc[:, 1:2])
+    w4 = act([w3], T.wc[:, 4:5], T.dl[:, 3:4], scale=-16.0, bias=T.wc[:, 3:4])
+    awz2 = act([vv], T.aw[:, NE:S], T.vv[:], scale=0.0)
+    bo = act([bd], T.bo[:], T.bd[:], scale=T.dl[:, 0:1])
+    rb = act([w4], T.rb[:], T.e0[:], scale=T.wc[:, 4:5])
+
+    att = dma("d_att", [awz, awz2], T.aw[0:128:16, :], T.opa[:])
+    for c in range(3):
+        att = dma("d_att", [], T.aw[4 + 4 * c:128:16, :], T.hue[c:24:3, :])
+
+    bank_free = [None, None]
+    rqo = [None] * 4
+    gb = None
+    for k in range(4):
+        o = P[6 + k % 2][:, 0:2 * LW]
+        b = SP + 2 * CAP * k
+        for p in range(16):
+            t = mm([sct, rw, bank_free[k % 2]], o, T.rw[:, 16 - p:144 - p], T.wn[:, b + p:b + 2 * CAP:16], p == 0, p == 15)
+        if k == 0:
+            gb = cp([geo], T.gb[:], T.gi[:])
+        for j in range(2):
+            i = 2 * k + j
+            out = T.rqi if ask[i] == rank else T.rqo
+            rqo[k] = ts([t], out[:, cols(i, LW)], P[6 + k % 2][:, cols(j, LW)],
+                        64.0 * S * ask[i], OP.subtract, 0.0, OP.max)
+        bank_free[k % 2] = rqo[k]
+
+    def rq_item(i, engs):
+        at = orders(T, topo, ask[i])[1].index(rank)
+        return (ask[i], engs, "rq%d" % (at // 2), T.rqo[:, cols(i, LW)], T.rqi[:, cols(at, LW)])
+
+    send([rqo[0]], [rq_item(0, far[:hf]), rq_item(1, far[hf:])])
+    send([rqo[1]], [rq_item(2, far[:hf]), rq_item(3, far[hf:])])
+    send([rqo[3]], [rq_item(4, far[:hf]), rq_item(5, far[hf:]), rq_item(6, near)])
+    rq_in = [("rq0", 2 * hf), ("rq1", 2 * hf), ("rq2", 2 * hf), ("rq3", len(near))]
+    idf = op("g", [onef], lambda e: e.affine_select(T.idf[:], T.onef[:], [[-1, 128]], OP.is_equal, 0.0, 0, 1))
+    selc = op("g", [one], lambda e: e.affine_select(T.selc[:], T.one[:, 0:24], [[-16, 8], [-4, 3]], OP.is_equal, 0.0, -4, 1))
+
+    for a in range(3):
+        att = dma("d_att", [gb], T.aw[1 + a:128:16, :], T.gb[:, cols(a, 256)])
+
+    fin = ts([ms], T.fin[:], T.ms[:, 7:1024:8], float(DUMP + SP - Z), OP.subtract)
+    gwz = fill([], T.gw[:, 0:Z + 6 * CAP], 0.0)
+
+    su, ga, gv, of, col, fa, fv, base = ([None] * 4 for _ in range(8))
+
+    def attr(k):
+        c2 = cols(k, 2 * LW)
+        su[k] = ts([rq_in[k], rqo[3]], T.su[:, c2], T.rqi[:, c2], 2.0 ** -6, OP.mult, 27.5 / 64, OP.subtract)
+        gv[k] = cp([su[k], att], T.gq[:, cols(2 * k + 1, CAP)], T.aw[:].indirect(T.su[:, cols(2 * k + 1, LW)]))
+        ga[k] = act([su[k], att], T.gq[:, cols(2 * k, CAP)], T.aw[:].indirect(T.su[:, cols(2 * k, LW)]))
+        of[k] = ts([], T.of[:, c2], T.rqi[:, c2], 63, OP.bitwise_and)
+        o = P[6 + k % 2][:, 0:2 * LW]
+        b = 2 * CAP * k
+        for p in range(16):
+            base[k] = mm([ga[k], gv[k], rb, bank_free[k % 2]], o, T.rb[:, 16 - p:144 - p],
+                         T.gq[:, b + p:b + 2 * CAP:16], p == 0, p == 15)
+
+    def foot(k):
+        c2 = cols(k, 2 * LW)
+        x = tt([base[k], of[k]], T.cf[:, c2], P[6 + k % 2][:, 0:2 * LW], T.of[:, c2], OP.add)
+        bank_free[k % 2] = x
+        col[k] = ts([x], T.cu[:, c2], T.cf[:, c2], 136.0, OP.add)
+        i = 2 * k + 1
+        out = T.fw[:, cols(7, CAP)] if serve[i] == rank else T.fq[:, cols(i, CAP)]
+        fv[k] = cp([col[k], dic], out, T.dw[:].indirect(T.cu[:, cols(i, LW)]))
+        fa[k] = act([col[k], dic], T.fq[:, cols(2 * k, CAP)], T.dw[:].indirect(T.cu[:, cols(2 * k, LW)]))
+
+    attr(0)
+    attr(1)
+    foot(0)
+    attr(2)
+    foot(1)
+    attr(3)
+    foot(2)
+    foot(3)
+
+    for i in range(6):
+        pk = dma("d_pk", [ga[i // 2], gv[i // 2]], T.gout[i], T.gq[0:128:4, cols(i, CAP)])
+
+    def place(r):
+        return orders(T, topo, r)[0].index(rank)
+
+    def f_item(i, engs):
+        at = place(serve[i])
+        return (serve[i], engs, "f%d" % (at // 2), T.fq[:, cols(i, CAP)], T.fw[:, cols(at, CAP)])
+
+    g_engs = [far[0:2], far[2:4]] + [[e] for e in far[4:8]]
+    send([fa[0], fv[0]], [f_item(0, far[:hf]), f_item(1, far[hf:])])
+    send([pk], [(serve[i], g_engs[i], "g_far", T.gout[i], T.gin[place(serve[i])]) for i in range(6)])
+    send([fa[1], fv[1]], [f_item(2, far[:hf]), f_item(3, far[hf:])])
+    send([fa[2], fv[2]], [f_item(4, far[:hf]), f_item(5, far[hf:])])
+    send([fa[3], ga[3]], [f_item(6, near[:hn]), (serve[6], near[hn:], "g_near", T.gq[:, cols(6, CAP)],
+                                                 T.gw[:, cols(place(serve[6]), CAP, Z)])])
+    g_far = ("g_far", sum(len(e) for e in g_engs))
+    g_near = ("g_near", len(near) - hn)
+    f_in = [("f0", 2 * hf)] * 2 + [("f1", 2 * hf)] * 2 + [("f2", 2 * hf)] * 2 + [("f3", hn), fv[3]]
+
+    un = dma("d_un", [gv[3]], T.gw[:, cols(7, CAP, Z)], T.gq[:, cols(7, CAP)])
+    for i in range(6):
+        un = dma("d_un", [g_far, gwz], T.gw[0:128:4, cols(i, CAP, Z)], T.gin[i])
+
+    alz = fill([], T.al[:, 0:Z], 0.0)
+    omz = fill([], T.om[:, 0:1], 1.0)
+    ctz = fill([], T.ct[:], 0.0)
+    st0 = fill([], T.st[:], 0.0)
+    k1 = ts([kc], T.kc[:, 1:2], T.kc[:, 0:1], 15, OP.bitwise_and, 1, OP.arith_shift_right)
+    k2 = ts([kc], T.kc[:, 2:3], T.kc[:, 0:1], 1, OP.bitwise_and)
+    k3 = ts([kc], T.kc[:, 3:4], T.kc[:, 0:1], 4, OP.arith_shift_right)
+    st = fill([st0], T.st[:, 0:256:64], 1.0)
+    f1 = ts([k1], T.kf[:, 0:1], T.kc[:, 1:2], 48.0, OP.mult)
+    f2 = ts([k3, f1], T.kf[:, 1:2], T.kc[:, 3:4], 6.0, OP.mult, T.kf[:, 0:1], OP.add)
+    f3 = ts([k2, f2], T.kf[:, 2:3], T.kc[:, 2:3], T.kf[:, 1:2], OP.add)
+    pick = ts([ip, f3], T.pick[:, 0:6], T.ip[:, 0:6], T.kf[:, 2:3], OP.add)
+
+    bank = {0: 0, 1: 1, 2: 2, 3: 3, 7: 5, 4: 6, 5: 7, 6: 0}
+    oa, al, ge = [None] * N, [None] * N, [None] * 4
+
+    def spread(i, deps):
+        oa[i] = mm([un, g_near, bo] + deps, P[bank[i]][:, 0:CAP], T.bo[:], T.gw[:, cols(i, CAP, Z)], True, True)
+
+    def alpha(i):
+        al[i] = tt([f_in[i], oa[i]], T.al[:, cols(i, CAP, Z)], P[bank[i]][:, 0:CAP], T.fw[:, cols(i, CAP)], OP.mult)
+
+    def colours(k, by):
+        ge[k] = by([un, g_near, gwz, fin], T.ge[:, cols(k, 512)], T.gw[:].indirect(T.fin[:, cols(k, 32)]))
+
+    for i in (0, 1, 2, 3, 7, 4, 5):
+        spread(i, [vv, ms, bank_free[0], bank_free[1]])
+    for k in range(3):
+        colours(k, act)
+    alpha(0)
+    spread(6, [al[0]])
+    alpha(1)
+    alpha(7)
+    colours(3, cp)
+    for i in (2, 3, 6, 4, 5):
+        alpha(i)
+    for b in range(16):
+        ctp = mm([selc, ge[b // 4]], P[4][:, cols(b, 24)], T.ge[:, cols(b, 128)], T.selc[:], True, True, b == 15)
+    act([ctp, ctz], T.ct[0:64, 0:768:2], P[4][0:64, 0:384])
+    ct = act([ctp, ctz], T.ct[64:128, 1:768:2], P[4][64:128, 0:384])
+
+    NC, W = 8, 256
+    om, li, ww, tr, wt, ym, ya = ([None] * NC for _ in range(7))
+    ready = [al[5], alz, fin]
+
+    def rest(k):
+        om[k] = act(ready + [omz], T.om[:, cols(k, W, 1)], T.al[:].indirect(T.fin[:, cols(k, W // 16)]),
+                    scale=-1.0, bias=1.0)
+
+    def light(k):
+        li[k] = op("v", [om[k], st], lambda e: e.tensor_tensor_scan(
+            T.li[:, cols(k, W)], T.om[:, cols(k, W)], T.st[:], 1.0, OP.mult, OP.max))
+
+    def weight(k):
+        ww[k] = tt(ready + [li[k]], T.ww[:, cols(k, W)], T.al[:].indirect(T.fin[:, cols(k, W // 16)]),
+                   T.li[:, cols(k, W)], OP.mult)
+        for h in range(2):
+            tr[k] = op("t", [ww[k], idf, wt[k - 2] if k > 1 else None], lambda e, h=h: e.transpose(
+                P[k % 2][:, cols(h, 128)], T.ww[:, cols(2 * k + h, 128)], T.idf[:]), h == 1)
+
+    def turn(k):
+        wt[k] = act([tr[k]], T.wt[:, cols(k, W)], P[k % 2][:, 0:W])
+
+    def sums(k):
+        for h in range(2):
+            b = 2 * k + h
+            ym[k] = mm([wt[k], ct, ya[k - 2] if k > 1 else None], P[2 + k % 2][:, cols(h, 48)],
+                       T.wt[:, cols(b, 128)], T.ct[:, cols(b, 48)], True, True, h == 1)
+
+    def out(k):
+        ya[k] = cp([ym[k]], T.ya[:, cols(k, 96)], P[2 + k % 2][:, 0:96])
+
+    rest(0)
+    rest(1)
+    light(0)
+    for k in range(NC + 2):
+        if k + 2 < NC:
+            rest(k + 2)
+        if k + 1 < NC:
+            light(k + 1)
+        if 0 <= k - 2 < NC:
+            out(k - 2)
+        if k < NC:
+            weight(k)
+        if 0 <= k - 1 < NC:
+            sums(k - 1)
+        if k < NC:
+            turn(k)
+    yo = cp([ya[NC - 1], pick], T.yo[:], T.ya[:].indirect(T.pick[:, 0:6]))
+    y = dma("d_y", [yo], T.y[:], T.yo[:])
+
+    wait("s", [y, ("d_pk", count["d_pk"])])
+    wait("g", [(s, count[s]) for s in ("cv", "ca", "ct", "cg", "sent")])

@@ -3,38 +3,41 @@ from concourse.mybir import AluOpType as OP, ActivationFunctionType as AF
 
 N, S, CAP, NE = 8, 4096, 320, 2048
 LW = CAP // 16
+FW = CAP // 4
+RW = CAP + FW
 Z = 16
-SP = NE + 128
+SP = NE + 128 + CAP
 BIG = 8192.0
 DUMP = 8192 - 1280 + 1 - SP
-UW = 132
 
 SCRATCH = {
     "ent_s": ("sbuf", [128, 128], "int32"),
-    "i1": ("sbuf", [128, 160], "int32"), "i1s": ("sbuf", [128, 160], "int32"), "e0": ("sbuf", [128, 160], "bfloat16"),
-    "i2": ("sbuf", [128, 16], "int32"), "i2s": ("sbuf", [128, 16], "int32"), "dl": ("sbuf", [128, 16], "float32"),
+    "zf": ("sbuf", [128, 160], "float32"), "zb": ("sbuf", [128, 512], "bfloat16"), "zh": ("sbuf", [128, 144], "float16"),
     "i3": ("sbuf", [128, 128], "int32"), "i3s": ("sbuf", [128, 128], "int32"),
     "bd": ("sbuf", [128, 128], "bfloat16"), "nbd": ("sbuf", [128, 128], "bfloat16"),
     "l0": ("sbuf", [128, 128], "bfloat16"), "l1": ("sbuf", [128, 128], "bfloat16"),
-    "offc": ("sbuf", [128, 128], "bfloat16"), "d0": ("sbuf", [128, 1024], "float32"),
-    "one": ("sbuf", [128, 128], "bfloat16"), "onef": ("sbuf", [128, 128], "float32"),
+    "tcon": ("sbuf", [128, 512], "bfloat16"), "d0": ("sbuf", [128, 1024], "float32"),
+    "one": ("sbuf", [128, 128], "bfloat16"), "sh": ("sbuf", [128, 144], "float16"), "sb": ("sbuf", [128, 144], "bfloat16"),
     "idf": ("sbuf", [128, 128], "float32"), "selc": ("sbuf", [128, 24], "bfloat16"),
-    "kc": ("sbuf", [128, 8], "int32"), "kf": ("sbuf", [128, 8], "float32"), "wc": ("sbuf", [128, 8], "float32"),
+    "kc": ("sbuf", [128, 8], "int32"), "kf": ("sbuf", [128, 8], "float32"),
     "ip": ("sbuf", [128, 8], "int32"), "pick": ("sbuf", [128, 8], "uint16"),
-    "um": ("sbuf", [128, 16 * UW], "bfloat16"),
-    "rw": ("sbuf", [128, 160], "bfloat16"), "rb": ("sbuf", [128, 160], "bfloat16"), "bo": ("sbuf", [128, 128], "bfloat16"),
-    "ob": ("sbuf", [128, 128], "bfloat16"), "hi": ("sbuf", [128, 128], "bfloat16"), "lo": ("sbuf", [128, 128], "bfloat16"),
+    "rb": ("sbuf", [128, 144], "bfloat16"), "fo": ("sbuf", [128, 144], "bfloat16"), "bo": ("sbuf", [128, 512], "bfloat16"),
+    "ob": ("sbuf", [128, 128], "bfloat16"), "si": ("sbuf", [128, 128], "int32"), "s16": ("sbuf", [128, 128], "float16"),
     "mk": ("sbuf", [128, 1024], "bfloat16"), "sc": ("sbuf", [128, 1024], "bfloat16"), "ms": ("sbuf", [128, 1024], "float32"),
     "slot": ("sbuf", [128, 128], "uint16"), "fin": ("sbuf", [128, 128], "uint16"),
-    "vv": ("sbuf", [128, NE], "bfloat16"), "wn": ("sbuf", [128, SP + N * CAP], "bfloat16"),
-    "rqo": ("sbuf", [128, N * LW], "int32"), "rqi": ("sbuf", [128, N * LW], "int32"),
-    "su": ("sbuf", [128, N * LW], "uint16"), "of": ("sbuf", [128, N * LW], "int32"),
-    "cf": ("sbuf", [128, N * LW], "float32"), "cu": ("sbuf", [128, N * LW], "uint16"),
+    "xd": ("sbuf", [128, 128], "int32"), "xp": ("sbuf", [128, 128], "int32"),
+    "xa": ("sbuf", [128, 128], "float32"), "xb": ("sbuf", [128, 128], "float32"), "xc": ("sbuf", [128, 128], "float32"),
+    "vv": ("sbuf", [128, NE], "float32"),
+    "wa": ("sbuf", [128, SP + N * CAP], "float32"), "wv": ("sbuf", [128, SP + N * CAP], "float32"),
+    "ra": ("dram", [N - 1, 128, LW], "float32"), "rv": ("dram", [N - 1, 128, LW], "float32"),
+    "rqa": ("sbuf", [128, LW], "float32"), "rqv": ("sbuf", [128, LW], "float32"), "rqi": ("sbuf", [128, N * LW], "float32"),
+    "su": ("sbuf", [128, N * LW], "uint16"), "vi": ("sbuf", [128, N * LW], "int32"),
+    "t31": ("sbuf", [128, N * LW], "int32"), "t24": ("sbuf", [128, N * LW], "int32"),
+    "of": ("sbuf", [128, N * LW], "bfloat16"), "cu": ("sbuf", [128, N * LW], "uint16"),
     "dw": ("sbuf", [128, S], "bfloat16"), "aw": ("sbuf", [128, S], "bfloat16"),
     "gi": ("sbuf", [128, 768], "int32"), "gb": ("sbuf", [128, 768], "bfloat16"),
-    "gq": ("sbuf", [128, N * CAP], "bfloat16"), "fq": ("sbuf", [128, N * CAP], "bfloat16"),
-    "gw": ("sbuf", [128, Z + N * CAP], "bfloat16"), "fw": ("sbuf", [128, N * CAP], "bfloat16"),
-    "gout": ("dram", [6, 128, CAP // 4], "bfloat16"), "gin": ("dram", [6, 128, CAP // 4], "bfloat16"),
+    "gq": ("sbuf", [128, N * CAP], "bfloat16"), "fq": ("sbuf", [128, N, RW], "bfloat16"),
+    "gw": ("sbuf", [128, Z + N * CAP], "bfloat16"), "fw": ("sbuf", [128, N - 1, RW], "bfloat16"),
     "ge": ("sbuf", [128, NE], "bfloat16"), "al": ("sbuf", [128, Z + N * CAP], "float32"),
     "ct": ("sbuf", [128, 768], "float32"), "st": ("sbuf", [128, 256], "bfloat16"),
     "om": ("sbuf", [128, NE + 4], "float32"), "li": ("sbuf", [128, NE], "float32"),
@@ -44,8 +47,8 @@ SCRATCH = {
 for _b in range(8):
     SCRATCH["p%d" % _b] = ("psum", [128, 512], "float32")
 
-SEMAPHORES = ["cv", "ca", "ct", "cg", "d_ent", "d_geo", "d_dic", "d_att", "d_pk", "d_un", "d_y",
-              "sent", "rq0", "rq1", "rq2", "rq3", "g_far", "g_near", "f0", "f1", "f2", "f3"]
+SEMAPHORES = ["cv", "ca", "ct", "cg", "d_ent", "d_wa", "d_wv", "d_geo", "d_dic", "d_att", "d_y", "lq0", "lq1", "lq2", "lq3",
+              "sent", "rq0", "rq1", "rq2", "rq3", "f0", "f1", "f2", "f3"]
 
 
 def orders(T, topo, rank):
@@ -87,9 +90,9 @@ def rank_program(g, core, T, topo):
         ins.then_inc(T.sem[s], 1)
         return (s, count[s])
 
-    def dma(s, deps, out, in_):
-        wait("s", deps)
-        g.sync.dma_start(out, in_).then_inc(T.sem[s], 16)
+    def dma(s, deps, out, in_, q="s"):
+        wait(q, deps)
+        Q[q].dma_start(out, in_).then_inc(T.sem[s], 16)
         count[s] = count.get(s, 0) + 16
         return (s, count[s])
 
@@ -107,17 +110,20 @@ def rank_program(g, core, T, topo):
     def fill(deps, out, c):
         return op("v", deps, lambda e: e.memset(out, c))
 
-    def act(deps, out, a, **kw):
-        f = AF.Identity if kw else AF.Copy
+    def act(deps, out, a, f=None, **kw):
+        f = f or (AF.Identity if kw else AF.Copy)
         return op("a", deps, lambda e: e.activation(out, a, f, **kw))
 
     def mm(deps, out, lhsT, rhs, start, stop, mark=None):
         return op("t", deps, lambda e: e.matmul(out, lhsT, rhs, start, stop), stop if mark is None else mark)
 
-    def iota(out, pattern, base, cm, small=False):
+    def iota(deps, out, pattern, base, cm, small=False):
         if small:
-            return op("g", [], lambda e: e.iota(out, pattern, base, cm, allow_small_or_imprecise_dtypes=True))
-        return op("g", [], lambda e: e.iota(out, pattern, base, cm))
+            return op("g", deps, lambda e: e.iota(out, pattern, base, cm, allow_small_or_imprecise_dtypes=True))
+        return op("g", deps, lambda e: e.iota(out, pattern, base, cm))
+
+    def mark(deps, out, in_, pattern, base, value):
+        return op("g", deps, lambda e: e.affine_select(out, in_, pattern, OP.not_equal, value, base, 1))
 
     def cols(i, w, at=0):
         return slice(at + w * i, at + w * i + w)
@@ -131,238 +137,222 @@ def rank_program(g, core, T, topo):
     def send(deps, items):
         wait("g", deps)
         trs = []
-        for r, engs, s, src, dst in items:
+        for r, engs, s, srcs, dst in items:
             rid, pid, _ = topo.addr(T.cores[r])
-            trs.append(RemoteDMATransfer(dst_ids=[DstId(rid=rid, pnc=pid)], dma_engine_mask=bits(engs),
-                                         remote_sem=T.sem[s], src=src, dst=dst))
+            trs.append(RemoteDMATransfer(dst_ids=[DstId(rid=rid, pnc=pid)], dma_engine_mask=bits(engs), remote_sem=T.sem[s],
+                                         srcs=srcs, dsts=[dst], alu_op=1 if len(srcs) > 1 else 0))
             count["sent"] = count.get("sent", 0) + len(engs)
         g.remote_dma_fused(trs, local_sem=T.sem["sent"])
 
     far = topo.engines(core, T.cores[ask[0]])
     near = [e for e in topo.engines(core, T.cores[ask[6]]) if e not in far]
-    hf, hn = len(far) // 2, len(near) // 2
+    hf = len(far) // 2
     P = [T["p%d" % b] for b in range(8)]
 
     ent = dma("d_ent", [], T.ent_s[:], T.ent[:])
+    zf = fill([], T.zf[:], 0.0)
+    zb = fill([], T.zb[:], 0.0)
+    zh = fill([], T.zh[:], 0.0)
+    one = fill([], T.one[:], 1.0)
     for a in range(3):
         geo = dma("d_geo", [], T.gi[:, cols(a, 256)], T.geo[a:24:3, :])
+    waz = dma("d_wa", [zf], T.wa[0:128:16, SP:SP + N * CAP], T.zf[:])
+    wvz = dma("d_wv", [zf], T.wv[0:128:16, SP:SP + N * CAP], T.zf[:])
+    for row, src in ((0, T.opa[:]), (14, T.opa[:]), (2, T.hue[0:24:3, :]), (4, T.hue[1:24:3, :]), (6, T.hue[2:24:3, :])):
+        dma("d_att", [], T.aw[row:128:16, :], src)
+    for a in range(4):
+        dma("d_att", [], T.aw[32 * a + 1:32 * a + 32:2, :], T.dic[:])
     for k in range(8):
         dic = dma("d_dic", [], T.dw[cols(k, 16), :], T.dic[:])
 
-    i1 = iota(T.i1[:], [[-16, 10], [256, 16]], 16, 1)
-    i2 = iota(T.i2[:], [[-1, 16]], 16, 1)
-    i3 = iota(T.i3[:], [[-16, 8], [0, 16]], 0, 1)
-    offc = iota(T.offc[:], [[16, 4], [1, 8], [0, 4]], 0, 0, True)
-    one = fill([], T.one[:], 1.0)
-    onef = fill([], T.onef[:], 1.0)
-    x1 = ts([i1], T.i1s[:], T.i1[:], 4, OP.arith_shift_right)
-    x2 = ts([i2], T.i2s[:], T.i2[:], 15, OP.bitwise_and)
-    e0 = ts([x1], T.e0[:], T.i1s[:], 0.0, OP.is_equal)
-    dl = ts([x2], T.dl[:], T.i2s[:], 0.0, OP.is_equal)
+    i3 = iota([], T.i3[:], [[-16, 8], [0, 16]], 0, 1)
+    tcon = iota([], T.tcon[0:1, :], [[1, 16], [0, 32]], 0, 0, True)
+    sh = mark([zh], T.sh[:], T.zh[:], [[-1, 144]], 0, 32.0)
     x3 = ts([i3], T.i3s[:], T.i3[:], 4, OP.arith_shift_right)
-    um = [None] * 16
-    um[0] = ts([e0, dl], T.um[:, 0:UW], T.e0[:, 14:14 + UW], T.dl[:, 0:1], OP.mult)
     nbd = ts([x3], T.nbd[:], T.i3s[:], 0.0, OP.is_equal, -1.0, OP.mult)
     bd = ts([x3], T.bd[:], T.i3s[:], 0.0, OP.is_equal)
-    for p in (4, 8, 12):
-        um[p] = ts([e0, dl], T.um[:, cols(p, UW)], T.e0[:, 14:14 + UW], T.dl[:, p:p + 1], OP.mult)
-    for b in range(1, 4):
-        for p in range(b, 16, 4):
-            um[p] = act([e0, dl], T.um[:, cols(p, UW)], T.e0[:, 14:14 + UW], scale=T.dl[:, p:p + 1])
     l0 = op("g", [nbd], lambda e: e.affine_select(T.l0[:], T.nbd[:], [[-1, 128]], OP.is_gt, 0.0, 0, 1))
-    l1 = op("g", [l0], lambda e: e.affine_select(T.l1[:], T.l0[:], [[-1, 128]], OP.not_equal, BIG, 0, 1))
-    d0 = iota(T.d0[:], [[-16, 128], [8192, 8]], DUMP + 16 * 127, 1, True)
-    kc = iota(T.kc[:, 0:1], [[0, 1]], 0, 1)
-    ip = iota(T.ip[:, 0:6], [[2, 3], [384, 2]], 0, 0)
-    awz = iota(T.aw[:, 0:NE], [[0, NE]], 0, 0, True)
+    l1 = mark([l0], T.l1[:], T.l0[:], [[-1, 128]], 0, BIG)
+    for h in range(2):
+        d0 = act([zb], T.d0[:, cols(h, 512)], T.zb[:], AF.Silu, bias=2 * BIG, scale=0.0)
+    d0 = iota([d0], T.d0[:, 0:1024:8], [[-16, 128]], DUMP + 16 * 127, 1, True)
 
-    magic = 1.5 * 2.0 ** 31
-    hi = ts([ent], T.hi[:], T.ent_s[:], magic, OP.add, magic, OP.subtract)
+    si = ts([ent], T.si[:], T.ent_s[:], S - 1, OP.bitwise_and)
     ob = ts([ent], T.ob[:], T.ent_s[:], 2.0 ** -12, OP.mult, 135.5 + 2.0 ** -13, OP.add)
-    lo = tt([hi], T.lo[:], T.ent_s[:], T.hi[:], OP.subtract)
+    s16 = ts([si], T.s16[:], T.si[:], float(S // 2), OP.subtract)
     mks = [ts([ob], T.mk[:, i:1024:8], T.ob[:], 136.0 + ask[i], OP.is_equal) for i in range(N)]
     scs = [op("v", [mks[i], one], lambda e, i=i: e.tensor_tensor_scan(
         T.sc[:, i:1024:8], T.one[:], T.mk[:, i:1024:8], 20.0 * (i - 4), OP.mult, OP.add)) for i in range(N)]
-    wnz = fill([], T.wn[:, SP:SP + N * CAP], 0.0)
 
-    unw = [None] * 4
-    cnt = [None, None]
-
-    def unwrap(b):
-        for j in range(4):
-            o = P[b][:, j:512:4]
-            u = UW * (b + 4 * j)
-            mm([um[b + 4 * j], offc], o, T.um[:, u:u + 128], T.offc[:], True, False)
-            mm([hi], o, T.um[:, u + 2:u + 130], T.hi[:], False, False)
-            unw[b] = mm([lo], o, T.um[:, u + 1:u + 129], T.lo[:], False, True, j == 3)
-
-    unwrap(0)
-    unwrap(1)
+    for b in range(4):
+        mm([tcon, one], P[b][:], T.one[0:1, :], T.tcon[0:1, :], True, False)
+    vv, cnt, slot = [None] * 4, [None] * 2, [None] * 2
+    for b in range(4):
+        h, odd = b // 2, b % 2
+        for j in range(8):
+            p = 2 * j + odd
+            t = mm([sh, s16], P[b][:, j:512:8], T.sh[:, p:p + 128], T.s16[:, cols(h, 64)], False, j == 7)
+        vv[b] = act([t], T.vv[:, 1024 * h + odd:1024 * h + 1024:2], P[b][:], bias=16.0 * S + 32 + 16 * h)
     for h in range(2):
         mm([mks[-1], l1], P[4 + h][:], T.l1[:], T.mk[:, cols(h, 512)], True, False)
-    unwrap(2)
     for h in range(2):
         cnt[h] = mm([scs[-1], bd], P[4 + h][:], T.bd[:], T.sc[:, cols(h, 512)], False, True)
-    unwrap(3)
-    for b in range(4):
-        vv = act([unw[b]], T.vv[:, b:NE:4], P[b][:])
-
     for h in range(2):
         ms = op("v", [cnt[h], d0], lambda e, h=h: e.tensor_tensor_scan(
             T.ms[:, cols(h, 512)], T.d0[:, cols(h, 512)], P[4 + h][:], 65536.0, OP.min, OP.max))
-    slot = ts([ms], T.slot[:], T.ms[:, 7:1024:8], float(DUMP), OP.subtract)
-    sct = cp([slot, vv, wnz], T.wn[:].indirect(T.slot[:]), T.vv[:])
+        slot[h] = ts([ms], T.slot[:, cols(h, 64)], T.ms[:, 512 * h + 7:512 * h + 512:8], float(DUMP), OP.subtract)
+    sa = act([slot[0], vv[1], waz], T.wa[:].indirect(T.slot[:, 0:64]), T.vv[:, 0:1024], AF.Silu)
+    sv = cp([slot[1], vv[3], wvz], T.wv[:].indirect(T.slot[:, 64:128]), T.vv[:, 1024:NE])
 
-    w0 = act([dl], T.wc[:, 0:1], T.dl[:, 0:1], scale=64.0, bias=T.dl[:, 2:3])
-    w2 = act([dl], T.wc[:, 2:3], T.dl[:, 2:3], scale=-1.0)
-    w1 = act([w0], T.wc[:, 1:2], T.dl[:, 1:2], scale=64.0, bias=T.wc[:, 0:1])
-    w3 = act([w2], T.wc[:, 3:4], T.dl[:, 1:2], scale=256.0, bias=T.wc[:, 2:3])
-    rw = act([w1], T.rw[:], T.e0[:], scale=T.wc[:, 1:2])
-    w4 = act([w3], T.wc[:, 4:5], T.dl[:, 3:4], scale=-16.0, bias=T.wc[:, 3:4])
-    awz2 = act([vv], T.aw[:, NE:S], T.vv[:], scale=0.0)
-    bo = act([bd], T.bo[:], T.bd[:], scale=T.dl[:, 0:1])
-    rb = act([w4], T.rb[:], T.e0[:], scale=T.wc[:, 4:5])
+    lq = [None] * 4
+    for q, win, dep, far_side, own_side in (("a", T.wa, sa, T.ra, T.rqa), ("s", T.wv, sv, T.rv, T.rqv)):
+        for i in range(N):
+            k = 3 if i == N - 1 else min(i // 2, 2)
+            lq[k] = dma("lq%d" % k, [dep], own_side[:] if k == 3 else far_side[i], win[0:128:16, cols(i, CAP, SP)], q)
 
-    att = dma("d_att", [awz, awz2], T.aw[0:128:16, :], T.opa[:])
-    for c in range(3):
-        att = dma("d_att", [], T.aw[4 + 4 * c:128:16, :], T.hue[c:24:3, :])
-
-    bank_free = [None, None]
-    rqo = [None] * 4
-    gb = None
-    for k in range(4):
-        o = P[6 + k % 2][:, 0:2 * LW]
-        b = SP + 2 * CAP * k
-        for p in range(16):
-            t = mm([sct, rw, bank_free[k % 2]], o, T.rw[:, 16 - p:144 - p], T.wn[:, b + p:b + 2 * CAP:16], p == 0, p == 15)
-        if k == 0:
-            gb = cp([geo], T.gb[:], T.gi[:])
-        for j in range(2):
-            i = 2 * k + j
-            out = T.rqi if ask[i] == rank else T.rqo
-            rqo[k] = ts([t], out[:, cols(i, LW)], P[6 + k % 2][:, cols(j, LW)],
-                        64.0 * S * ask[i], OP.subtract, 0.0, OP.max)
-        bank_free[k % 2] = rqo[k]
+    rb = mark([zb], T.rb[:], T.zb[:, 0:144], [[-16, 9], [1000, 16]], 16 - 8, 256.0)
+    rb = mark([rb], T.rb[:], T.rb[:], [[-16, 9], [1000, 16]], 16 - 10, -1.0)
+    rb = mark([rb], T.rb[:], T.rb[:], [[-16, 9], [1000, 16]], 16 - 12, -16.0)
+    sb = mark([], T.sb[:], T.zb[:, 0:144], [[-1, 144]], 0, 1.0)
+    fo = mark([], T.fo[:], T.zb[:, 0:144], [[-16, 9], [-2, 4], [-1000, 4]], 3000, 1.0)
+    bo = mark([], T.bo[:], T.zb[:], [[-1, 4], [-16, 8], [0, 16]], 0, 1.0)
+    idf = mark([zf], T.idf[:], T.zf[:, 0:128], [[-1, 128]], 0, 1.0)
+    selc = mark([], T.selc[:], T.zb[:, 0:24], [[-16, 8], [-4, 3]], -4, 1.0)
+    kc = iota([], T.kc[:, 0:1], [[0, 1]], 0, 1)
+    ip = iota([], T.ip[:, 0:6], [[2, 3], [384, 2]], 0, 0)
 
     def rq_item(i, engs):
         at = orders(T, topo, ask[i])[1].index(rank)
-        return (ask[i], engs, "rq%d" % (at // 2), T.rqo[:, cols(i, LW)], T.rqi[:, cols(at, LW)])
+        return (ask[i], engs, "rq%d" % (at // 2), [T.ra[i], T.rv[i]], T.rqi[:, cols(at, LW)])
 
-    send([rqo[0]], [rq_item(0, far[:hf]), rq_item(1, far[hf:])])
-    send([rqo[1]], [rq_item(2, far[:hf]), rq_item(3, far[hf:])])
-    send([rqo[3]], [rq_item(4, far[:hf]), rq_item(5, far[hf:]), rq_item(6, near)])
+    send([lq[0]], [rq_item(0, far[:hf]), rq_item(1, far[hf:])])
+    send([lq[1]], [rq_item(2, far[:hf]), rq_item(3, far[hf:])])
+    send([lq[2]], [rq_item(4, far[:hf]), rq_item(5, far[hf:]), rq_item(6, near)])
     rq_in = [("rq0", 2 * hf), ("rq1", 2 * hf), ("rq2", 2 * hf), ("rq3", len(near))]
-    idf = op("g", [onef], lambda e: e.affine_select(T.idf[:], T.onef[:], [[-1, 128]], OP.is_equal, 0.0, 0, 1))
-    selc = op("g", [one], lambda e: e.affine_select(T.selc[:], T.one[:, 0:24], [[-16, 8], [-4, 3]], OP.is_equal, 0.0, -4, 1))
 
+    gb = cp([geo], T.gb[:], T.gi[:])
     for a in range(3):
-        att = dma("d_att", [gb], T.aw[1 + a:128:16, :], T.gb[:, cols(a, 256)])
+        att = dma("d_att", [gb], T.aw[8 + 2 * a:128:16, :], T.gb[:, cols(a, 256)])
 
-    fin = ts([ms], T.fin[:], T.ms[:, 7:1024:8], float(DUMP + SP - Z), OP.subtract)
-    gwz = fill([], T.gw[:, 0:Z + 6 * CAP], 0.0)
+    at0 = float(DUMP + SP)
+    m7 = T.ms[:, 7:1024:8]
+    xd = ts([], T.xd[:], m7, at0 + 9.5, OP.subtract, 0.05, OP.mult)
+    xa = ts([], T.xa[:], m7, at0 - Z // 16, OP.subtract, 16.0, OP.mult)
+    xp = ts([xd], T.xp[:], T.xd[:], 15, OP.bitwise_and)
+    xb = ts([xd], T.xb[:], T.xd[:], -300.0, OP.mult)
+    xc = ts([xp], T.xc[:], T.xp[:], -19.0, OP.mult)
+    xa = tt([xa, xb], T.xa[:], T.xa[:], T.xb[:], OP.add)
+    k1 = ts([kc], T.kc[:, 1:2], T.kc[:, 0:1], 15, OP.bitwise_and, 1, OP.arith_shift_right)
+    xa = tt([xa, xc], T.xa[:], T.xa[:], T.xc[:], OP.add)
+    k2 = ts([kc], T.kc[:, 2:3], T.kc[:, 0:1], 1, OP.bitwise_and)
+    fin = cp([xa], T.fin[:], T.xa[:])
+    rqo = tt([lq[3]], T.rqi[:, cols(N - 1, LW)], T.rqa[:], T.rqv[:], OP.add)
 
-    su, ga, gv, of, col, fa, fv, base = ([None] * 4 for _ in range(8))
+    k3 = ts([kc], T.kc[:, 3:4], T.kc[:, 0:1], 4, OP.arith_shift_right)
+    gwz = fill([], T.gw[:, 0:Z], 0.0)
+    alz = fill([], T.al[:, 0:Z], 0.0)
+    omz = fill([], T.om[:, 0:1], 1.0)
+    st0 = fill([], T.st[:], 0.0)
+    f1 = ts([k1], T.kf[:, 0:1], T.kc[:, 1:2], 48.0, OP.mult)
+    st = fill([st0], T.st[:, 0:256:64], 1.0)
+    f2 = ts([k3, f1], T.kf[:, 1:2], T.kc[:, 3:4], 6.0, OP.mult, T.kf[:, 0:1], OP.add)
+    f3 = ts([k2, f2], T.kf[:, 2:3], T.kc[:, 2:3], T.kf[:, 1:2], OP.add)
+    pick = ts([ip, f3], T.pick[:, 0:6], T.ip[:, 0:6], T.kf[:, 2:3], OP.add)
+    act([zb], T.ct[:, 0:384], T.zb[:, 0:384])
+    ctz = act([zb], T.ct[:, 384:768], T.zb[:, 0:384])
 
-    def attr(k):
-        c2 = cols(k, 2 * LW)
-        su[k] = ts([rq_in[k], rqo[3]], T.su[:, c2], T.rqi[:, c2], 2.0 ** -6, OP.mult, 27.5 / 64, OP.subtract)
-        gv[k] = cp([su[k], att], T.gq[:, cols(2 * k + 1, CAP)], T.aw[:].indirect(T.su[:, cols(2 * k + 1, LW)]))
-        ga[k] = act([su[k], att], T.gq[:, cols(2 * k, CAP)], T.aw[:].indirect(T.su[:, cols(2 * k, LW)]))
-        of[k] = ts([], T.of[:, c2], T.rqi[:, c2], 63, OP.bitwise_and)
-        o = P[6 + k % 2][:, 0:2 * LW]
-        b = 2 * CAP * k
-        for p in range(16):
-            base[k] = mm([ga[k], gv[k], rb, bank_free[k % 2]], o, T.rb[:, 16 - p:144 - p],
-                         T.gq[:, b + p:b + 2 * CAP:16], p == 0, p == 15)
-
-    def foot(k):
-        c2 = cols(k, 2 * LW)
-        x = tt([base[k], of[k]], T.cf[:, c2], P[6 + k % 2][:, 0:2 * LW], T.of[:, c2], OP.add)
-        bank_free[k % 2] = x
-        col[k] = ts([x], T.cu[:, c2], T.cf[:, c2], 136.0, OP.add)
-        i = 2 * k + 1
-        out = T.fw[:, cols(7, CAP)] if serve[i] == rank else T.fq[:, cols(i, CAP)]
-        fv[k] = cp([col[k], dic], out, T.dw[:].indirect(T.cu[:, cols(i, LW)]))
-        fa[k] = act([col[k], dic], T.fq[:, cols(2 * k, CAP)], T.dw[:].indirect(T.cu[:, cols(2 * k, LW)]))
-
-    attr(0)
-    attr(1)
-    foot(0)
-    attr(2)
-    foot(1)
-    attr(3)
-    foot(2)
-    foot(3)
-
-    for i in range(6):
-        pk = dma("d_pk", [ga[i // 2], gv[i // 2]], T.gout[i], T.gq[0:128:4, cols(i, CAP)])
+    su, ga, gv, of, col, fa, fv, base, fold, fe = ([None] * 4 for _ in range(10))
 
     def place(r):
         return orders(T, topo, r)[0].index(rank)
 
     def f_item(i, engs):
         at = place(serve[i])
-        return (serve[i], engs, "f%d" % (at // 2), T.fq[:, cols(i, CAP)], T.fw[:, cols(at, CAP)])
+        return (serve[i], engs, "f%d" % (at // 2), [T.fq[:, i, :]], T.fw[:, at, :])
 
-    g_engs = [far[0:2], far[2:4]] + [[e] for e in far[4:8]]
-    send([fa[0], fv[0]], [f_item(0, far[:hf]), f_item(1, far[hf:])])
-    send([pk], [(serve[i], g_engs[i], "g_far", T.gout[i], T.gin[place(serve[i])]) for i in range(6)])
-    send([fa[1], fv[1]], [f_item(2, far[:hf]), f_item(3, far[hf:])])
-    send([fa[2], fv[2]], [f_item(4, far[:hf]), f_item(5, far[hf:])])
-    send([fa[3], ga[3]], [f_item(6, near[:hn]), (serve[6], near[hn:], "g_near", T.gq[:, cols(6, CAP)],
-                                                 T.gw[:, cols(place(serve[6]), CAP, Z)])])
-    g_far = ("g_far", sum(len(e) for e in g_engs))
-    g_near = ("g_near", len(near) - hn)
-    f_in = [("f0", 2 * hf)] * 2 + [("f1", 2 * hf)] * 2 + [("f2", 2 * hf)] * 2 + [("f3", hn), fv[3]]
+    def attr(k):
+        c2 = cols(k, 2 * LW)
+        su[k] = ts([rq_in[k], rqo], T.su[:, c2], T.rqi[:, c2], 47.5, OP.subtract, 2.0 ** -5, OP.mult)
+        gv[k] = cp([su[k], att], T.gq[:, cols(2 * k + 1, CAP)], T.aw[:].indirect(T.su[:, cols(2 * k + 1, LW)]))
+        ga[k] = act([su[k], att], T.gq[:, cols(2 * k, CAP)], T.aw[:].indirect(T.su[:, cols(2 * k, LW)]))
 
-    un = dma("d_un", [gv[3]], T.gw[:, cols(7, CAP, Z)], T.gq[:, cols(7, CAP)])
-    for i in range(6):
-        un = dma("d_un", [g_far, gwz], T.gw[0:128:4, cols(i, CAP, Z)], T.gin[i])
+    def offsets(k0, k1):
+        c = slice(2 * LW * k0, 2 * LW * k1)
+        vi = cp([rq_in[k] for k in range(k0, k1)] + [rqo], T.vi[:, c], T.rqi[:, c])
+        a = ts([vi], T.t31[:, c], T.vi[:, c], 31, OP.bitwise_and)
+        b = ts([vi], T.t24[:, c], T.vi[:, c], 24, OP.bitwise_and)
+        x = tt([a, b], T.of[:, c], T.t31[:, c], T.t24[:, c], OP.add)
+        for k in range(k0, k1):
+            of[k] = x
 
-    alz = fill([], T.al[:, 0:Z], 0.0)
-    omz = fill([], T.om[:, 0:1], 1.0)
-    ctz = fill([], T.ct[:], 0.0)
-    st0 = fill([], T.st[:], 0.0)
-    k1 = ts([kc], T.kc[:, 1:2], T.kc[:, 0:1], 15, OP.bitwise_and, 1, OP.arith_shift_right)
-    k2 = ts([kc], T.kc[:, 2:3], T.kc[:, 0:1], 1, OP.bitwise_and)
-    k3 = ts([kc], T.kc[:, 3:4], T.kc[:, 0:1], 4, OP.arith_shift_right)
-    st = fill([st0], T.st[:, 0:256:64], 1.0)
-    f1 = ts([k1], T.kf[:, 0:1], T.kc[:, 1:2], 48.0, OP.mult)
-    f2 = ts([k3, f1], T.kf[:, 1:2], T.kc[:, 3:4], 6.0, OP.mult, T.kf[:, 0:1], OP.add)
-    f3 = ts([k2, f2], T.kf[:, 2:3], T.kc[:, 2:3], T.kf[:, 1:2], OP.add)
-    pick = ts([ip, f3], T.pick[:, 0:6], T.ip[:, 0:6], T.kf[:, 2:3], OP.add)
+    def lists(k):
+        o = P[6 + k % 2][:, 0:2 * LW]
+        b = 2 * CAP * k
+        for p in range(16):
+            mm([ga[k], gv[k], rb, col[k - 2] if k > 1 else None], o, T.rb[:, 16 - p:144 - p],
+               T.gq[:, b + p:b + 2 * CAP:16], p == 0, False)
+        base[k] = mm([of[k], sb], o, T.sb[:, 0:128], T.of[:, cols(k, 2 * LW)], False, True)
+        for j in range(2):
+            for h in range(4):
+                fold[k] = mm([fo, ms, fe[k - 2] if k > 1 else None], P[4 + k % 2][:, cols(j, FW)], T.fo[:, 3 - h:131 - h],
+                             T.gq[:, cols(h, FW, b + CAP * j)], h == 0, h == 3, h == 3 and j == 1)
 
-    bank = {0: 0, 1: 1, 2: 2, 3: 3, 7: 5, 4: 6, 5: 7, 6: 0}
-    oa, al, ge = [None] * N, [None] * N, [None] * 4
+    def foot(k):
+        c2 = cols(k, 2 * LW)
+        col[k] = ts([base[k]], T.cu[:, c2], P[6 + k % 2][:, 0:2 * LW], 136.0, OP.add)
+        fv[k] = cp([col[k], dic], T.fq[:, 2 * k + 1, 0:CAP], T.dw[:].indirect(T.cu[:, cols(2 * k + 1, LW)]))
+        fa[k] = act([col[k], dic], T.fq[:, 2 * k, 0:CAP], T.dw[:].indirect(T.cu[:, cols(2 * k, LW)]))
+        fe[k] = act([fold[k]], T.fq[:, 2 * k:2 * k + 2, CAP:RW], P[4 + k % 2][:, 0:2 * FW])
+        if k < 3:
+            send([fv[k], fe[k]], [f_item(2 * k, far[:hf]), f_item(2 * k + 1, far[hf:])])
+        else:
+            send([fe[k]], [f_item(2 * k, near)])
 
-    def spread(i, deps):
-        oa[i] = mm([un, g_near, bo] + deps, P[bank[i]][:, 0:CAP], T.bo[:], T.gw[:, cols(i, CAP, Z)], True, True)
+    attr(0)
+    offsets(0, 1)
+    lists(0)
+    attr(1)
+    offsets(1, 4)
+    lists(1)
+    foot(0)
+    attr(2)
+    lists(2)
+    foot(1)
+    attr(3)
+    lists(3)
+    foot(2)
+    foot(3)
+    f_in = [[("f0", 2 * hf)]] * 2 + [[("f1", 2 * hf)]] * 2 + [[("f2", 2 * hf)]] * 2 + [[("f3", len(near))], [fv[3], fe[3]]]
 
-    def alpha(i):
-        al[i] = tt([f_in[i], oa[i]], T.al[:, cols(i, CAP, Z)], P[bank[i]][:, 0:CAP], T.fw[:, cols(i, CAP)], OP.mult)
-
-    def colours(k, by):
-        ge[k] = by([un, g_near, gwz, fin], T.ge[:, cols(k, 512)], T.gw[:].indirect(T.fin[:, cols(k, 32)]))
-
-    for i in (0, 1, 2, 3, 7, 4, 5):
-        spread(i, [vv, ms, bank_free[0], bank_free[1]])
-    for k in range(3):
-        colours(k, act)
-    alpha(0)
-    spread(6, [al[0]])
-    alpha(1)
-    alpha(7)
-    colours(3, cp)
-    for i in (2, 3, 6, 4, 5):
-        alpha(i)
-    for b in range(16):
-        ctp = mm([selc, ge[b // 4]], P[4][:, cols(b, 24)], T.ge[:, cols(b, 128)], T.selc[:], True, True, b == 15)
-    act([ctp, ctz], T.ct[0:64, 0:768:2], P[4][0:64, 0:384])
-    ct = act([ctp, ctz], T.ct[64:128, 1:768:2], P[4][64:128, 0:384])
+    al, un = [], []
+    for n, i in enumerate((0, 1, 7, 2, 3, 6, 4, 5)):
+        def got(c, i=i):
+            return T.fq[:, i, c] if i == N - 1 else T.fw[:, i, c]
+        for h in range(4):
+            a = mm(f_in[i] + [bo, vv[3], al[n - 2] if n > 1 else None], P[n % 2][:, cols(h, FW)], T.bo[:, cols(h, 128)],
+                   got(slice(CAP, RW)), True, True, h == 3)
+        for h in range(4):
+            u = mm([un[n - 2] if n > 1 else None], P[2 + n % 2][:, cols(h, FW)], T.sb[:, h:h + 128],
+                   got(slice(CAP, RW)), True, True, h == 3)
+        al.append(tt(f_in[i] + [a], T.al[:, cols(i, CAP, Z)], P[n % 2][:, 0:CAP], got(slice(0, CAP)), OP.mult))
+        un.append(act([u], T.gw[:, cols(i, CAP, Z)], P[2 + n % 2][:, 0:CAP]))
 
     NC, W = 8, 256
     om, li, ww, tr, wt, ym, ya = ([None] * NC for _ in range(7))
-    ready = [al[5], alz, fin]
+    ge, ctp, ct = ([None] * 4 for _ in range(3))
+    ready = [al[-1], alz, fin]
+
+    def colours(k, by):
+        ge[k] = by([un[-1], gwz, fin], T.ge[:, cols(k, 512)], T.gw[:].indirect(T.fin[:, cols(k, 32)]))
+
+    def turn_colours(k):
+        for b in range(4):
+            ctp[k] = mm([selc, ge[k], fe[3], ct[k - 2] if k > 1 else None], P[4 + k % 2][:, cols(b, 24)],
+                        T.ge[:, cols(4 * k + b, 128)], T.selc[:], True, True, b == 3)
+
+    def split_colours(k):
+        act([ctp[k], ctz], T.ct[0:64, 192 * k:192 * k + 192:2], P[4 + k % 2][0:64, 0:96])
+        ct[k] = act([], T.ct[64:128, 192 * k + 1:192 * k + 192:2], P[4 + k % 2][64:128, 0:96])
 
     def rest(k):
         om[k] = act(ready + [omz], T.om[:, cols(k, W, 1)], T.al[:].indirect(T.fin[:, cols(k, W // 16)]),
@@ -375,40 +365,50 @@ def rank_program(g, core, T, topo):
     def weight(k):
         ww[k] = tt(ready + [li[k]], T.ww[:, cols(k, W)], T.al[:].indirect(T.fin[:, cols(k, W // 16)]),
                    T.li[:, cols(k, W)], OP.mult)
-        for h in range(2):
-            tr[k] = op("t", [ww[k], idf, wt[k - 2] if k > 1 else None], lambda e, h=h: e.transpose(
-                P[k % 2][:, cols(h, 128)], T.ww[:, cols(2 * k + h, 128)], T.idf[:]), h == 1)
 
     def turn(k):
-        wt[k] = act([tr[k]], T.wt[:, cols(k, W)], P[k % 2][:, 0:W])
+        for h in range(2):
+            tr[k] = op("t", [ww[k], idf, col[3], wt[k - 4] if k > 3 else None], lambda e, h=h: e.transpose(
+                P[(0, 1, 6, 7)[k % 4]][:, cols(h, 128)], T.ww[:, cols(2 * k + h, 128)], T.idf[:]), h == 1)
+
+    def take(k):
+        wt[k] = act([tr[k]], T.wt[:, cols(k, W)], P[(0, 1, 6, 7)[k % 4]][:, 0:W])
 
     def sums(k):
         for h in range(2):
             b = 2 * k + h
-            ym[k] = mm([wt[k], ct, ya[k - 2] if k > 1 else None], P[2 + k % 2][:, cols(h, 48)],
+            ym[k] = mm([wt[k], ct[k // 2], un[-1], ya[k - 2] if k > 1 else None], P[2 + k % 2][:, cols(h, 48)],
                        T.wt[:, cols(b, 128)], T.ct[:, cols(b, 48)], True, True, h == 1)
 
     def out(k):
         ya[k] = cp([ym[k]], T.ya[:, cols(k, 96)], P[2 + k % 2][:, 0:96])
 
-    rest(0)
-    rest(1)
+    colours(0, cp)
+    for k in range(3):
+        rest(k)
+    turn_colours(0)
     light(0)
-    for k in range(NC + 2):
-        if k + 2 < NC:
-            rest(k + 2)
+    for k in range(NC + 3):
         if k + 1 < NC:
             light(k + 1)
-        if 0 <= k - 2 < NC:
-            out(k - 2)
         if k < NC:
             weight(k)
-        if 0 <= k - 1 < NC:
-            sums(k - 1)
-        if k < NC:
             turn(k)
+        if 0 <= k - 3 < NC:
+            out(k - 3)
+        if k + 3 < NC:
+            rest(k + 3)
+        if k in (1, 3, 5):
+            colours((k + 1) // 2, cp if k == 3 else act)
+            turn_colours((k + 1) // 2)
+        if k in (1, 3, 5, 7):
+            split_colours(k // 2)
+        if 0 <= k - 1 < NC:
+            take(k - 1)
+        if 0 <= k - 2 < NC:
+            sums(k - 2)
     yo = cp([ya[NC - 1], pick], T.yo[:], T.ya[:].indirect(T.pick[:, 0:6]))
     y = dma("d_y", [yo], T.y[:], T.yo[:])
 
-    wait("s", [y, ("d_pk", count["d_pk"])])
+    wait("s", [y])
     wait("g", [(s, count[s]) for s in ("cv", "ca", "ct", "cg", "sent")])

@@ -6,9 +6,14 @@ LW = CAP // 16
 FW = CAP // 4
 RW = CAP + FW
 Z = 16
-SP = NE + 128 + CAP
+SP = NE // 2 + 128 + CAP
+CUT = 70
 BIG = 8192.0
 DUMP = 8192 - 1280 + 1 - SP
+
+PLAN = {"v": "G04 L02 L24 W02 W24 L48 W46 W68 L8c W8a Lcg Wac Wce Wef X4a K8c Wfg O04 Kef Kfg Oae",
+        "a": "R02 R24 R48 X04 R8c Rcg K04 G4a Gag K48 Xag Kce O4a Oeg",
+        "t": "C04 T02 T24 T46 T68 M04 T8a C4a Tac Tce Tef Cag M8a Tfg M48 Mac Mce Mef Mfg"}
 
 SCRATCH = {
     "ent_s": ("sbuf", [128, 128], "int32"),
@@ -16,7 +21,7 @@ SCRATCH = {
     "i3": ("sbuf", [128, 128], "int32"), "i3s": ("sbuf", [128, 128], "int32"),
     "bd": ("sbuf", [128, 128], "bfloat16"), "nbd": ("sbuf", [128, 128], "bfloat16"),
     "l0": ("sbuf", [128, 128], "bfloat16"), "l1": ("sbuf", [128, 128], "bfloat16"),
-    "tcon": ("sbuf", [128, 512], "bfloat16"), "d0": ("sbuf", [128, 1024], "float32"),
+    "tcon": ("sbuf", [128, 512], "bfloat16"), "d0": ("sbuf", [128, 512], "float32"),
     "one": ("sbuf", [128, 128], "bfloat16"), "sh": ("sbuf", [128, 144], "float16"), "sb": ("sbuf", [128, 144], "bfloat16"),
     "idf": ("sbuf", [128, 128], "float32"), "selc": ("sbuf", [128, 24], "bfloat16"),
     "kc": ("sbuf", [128, 8], "int32"), "kf": ("sbuf", [128, 8], "float32"),
@@ -24,22 +29,21 @@ SCRATCH = {
     "rb": ("sbuf", [128, 144], "bfloat16"), "fo": ("sbuf", [128, 144], "bfloat16"), "bo": ("sbuf", [128, 512], "bfloat16"),
     "ob": ("sbuf", [128, 128], "bfloat16"), "si": ("sbuf", [128, 128], "int32"), "s16": ("sbuf", [128, 128], "float16"),
     "mk": ("sbuf", [128, 1024], "bfloat16"), "sc": ("sbuf", [128, 1024], "bfloat16"), "ms": ("sbuf", [128, 1024], "float32"),
-    "slot": ("sbuf", [128, 128], "uint16"), "fin": ("sbuf", [128, 128], "uint16"),
+    "rs": ("sbuf", [128, 1024], "bfloat16"), "slot": ("sbuf", [128, 128], "uint16"), "fin": ("sbuf", [128, 128], "uint16"),
     "xd": ("sbuf", [128, 128], "int32"), "xp": ("sbuf", [128, 128], "int32"),
     "xa": ("sbuf", [128, 128], "float32"), "xb": ("sbuf", [128, 128], "float32"), "xc": ("sbuf", [128, 128], "float32"),
     "vv": ("sbuf", [128, NE], "float32"),
     "wa": ("sbuf", [128, SP + N * CAP], "float32"), "wv": ("sbuf", [128, SP + N * CAP], "float32"),
     "ra": ("dram", [N - 1, 128, LW], "float32"), "rv": ("dram", [N - 1, 128, LW], "float32"),
     "rqa": ("sbuf", [128, LW], "float32"), "rqv": ("sbuf", [128, LW], "float32"), "rqi": ("sbuf", [128, N * LW], "float32"),
-    "su": ("sbuf", [128, N * LW], "uint16"), "vi": ("sbuf", [128, N * LW], "int32"),
-    "t31": ("sbuf", [128, N * LW], "int32"), "t24": ("sbuf", [128, N * LW], "int32"),
-    "of": ("sbuf", [128, N * LW], "bfloat16"), "cu": ("sbuf", [128, N * LW], "uint16"),
+    "su": ("sbuf", [128, N * LW], "uint16"), "r8": ("sbuf", [128, N * LW], "float32"),
+    "s64": ("sbuf", [128, N * LW], "float32"), "cu": ("sbuf", [128, N * LW], "uint16"),
     "dw": ("sbuf", [128, S], "bfloat16"), "aw": ("sbuf", [128, S], "bfloat16"),
     "gi": ("sbuf", [128, 768], "int32"), "gb": ("sbuf", [128, 768], "bfloat16"),
     "gq": ("sbuf", [128, N * CAP], "bfloat16"), "fq": ("sbuf", [128, N, RW], "bfloat16"),
     "gw": ("sbuf", [128, Z + N * CAP], "bfloat16"), "fw": ("sbuf", [128, N - 1, RW], "bfloat16"),
     "ge": ("sbuf", [128, NE], "bfloat16"), "al": ("sbuf", [128, Z + N * CAP], "float32"),
-    "ct": ("sbuf", [128, 768], "float32"), "st": ("sbuf", [128, 256], "bfloat16"),
+    "ct": ("sbuf", [128, 768], "float32"), "st": ("sbuf", [128, 512], "bfloat16"),
     "om": ("sbuf", [128, NE + 4], "float32"), "li": ("sbuf", [128, NE], "float32"),
     "ww": ("sbuf", [128, NE], "float32"), "wt": ("sbuf", [128, NE], "float32"),
     "ya": ("sbuf", [128, 768], "float32"), "yo": ("sbuf", [128, 96], "float32"),
@@ -48,13 +52,15 @@ for _b in range(8):
     SCRATCH["p%d" % _b] = ("psum", [128, 512], "float32")
 
 SEMAPHORES = ["cv", "ca", "ct", "cg", "d_ent", "d_wa", "d_wv", "d_geo", "d_dic", "d_att", "d_y", "lq0", "lq1", "lq2", "lq3",
-              "sent", "rq0", "rq1", "rq2", "rq3", "f0", "f1", "f2", "f3"]
+              "sent", "rq0", "rq1", "rq2", "rq3", "f0", "f1", "f2", "f3", "f4"]
 
 
 def orders(T, topo, rank):
     chips = sorted(set(topo.chip(c) for c in T.cores))
     on = [[r for r in range(N) if topo.chip(T.cores[r]) == ch] for ch in chips]
     a = chips.index(topo.chip(T.cores[rank]))
+    j = on[a].index(rank)
+    on = [x[j:] + x[:j] for x in on]
     tail = [r for r in on[a] if r != rank] + [rank]
     ask = [r for k in range(1, len(chips)) for r in on[(a - k) % len(chips)]] + tail
     serve = [r for k in range(1, len(chips)) for r in on[(a + k) % len(chips)]] + tail
@@ -171,38 +177,56 @@ def rank_program(g, core, T, topo):
     x3 = ts([i3], T.i3s[:], T.i3[:], 4, OP.arith_shift_right)
     nbd = ts([x3], T.nbd[:], T.i3s[:], 0.0, OP.is_equal, -1.0, OP.mult)
     bd = ts([x3], T.bd[:], T.i3s[:], 0.0, OP.is_equal)
+    rs = fill([], T.rs[:], 1024.0)
     l0 = op("g", [nbd], lambda e: e.affine_select(T.l0[:], T.nbd[:], [[-1, 128]], OP.is_gt, 0.0, 0, 1))
     l1 = mark([l0], T.l1[:], T.l0[:], [[-1, 128]], 0, BIG)
-    for h in range(2):
-        d0 = act([zb], T.d0[:, cols(h, 512)], T.zb[:], AF.Silu, bias=2 * BIG, scale=0.0)
-    d0 = iota([d0], T.d0[:, 0:1024:8], [[-16, 128]], DUMP + 16 * 127, 1, True)
+    rs = iota([rs], T.rs[:, 0:1024:128], [[-20, 8]], 60, 0, True)
+    d0 = act([zb], T.d0[:], T.zb[:], AF.Silu, bias=2 * BIG, scale=0.0)
+    d0 = iota([d0], T.d0[:, 0:512:8], [[-16, 64]], DUMP + 16 * 63, 1, True)
 
     si = ts([ent], T.si[:], T.ent_s[:], S - 1, OP.bitwise_and)
     ob = ts([ent], T.ob[:], T.ent_s[:], 2.0 ** -12, OP.mult, 135.5 + 2.0 ** -13, OP.add)
     s16 = ts([si], T.s16[:], T.si[:], float(S // 2), OP.subtract)
-    mks = [ts([ob], T.mk[:, i:1024:8], T.ob[:], 136.0 + ask[i], OP.is_equal) for i in range(N)]
-    scs = [op("v", [mks[i], one], lambda e, i=i: e.tensor_tensor_scan(
-        T.sc[:, i:1024:8], T.one[:], T.mk[:, i:1024:8], 20.0 * (i - 4), OP.mult, OP.add)) for i in range(N)]
+    mks = [ts([ob], T.mk[:, cols(j, 128)], T.ob[:], 136.0 + ask[N - 1 - j], OP.is_equal) for j in range(N)]
+    scs = [op("v", [mks[4 * h + 3], rs], lambda e, h=h: e.tensor_tensor_scan(
+        T.sc[:, cols(h, 512)], T.rs[:, cols(h, 512)], T.mk[:, cols(h, 512)], 1024.0, OP.min, OP.add)) for h in range(2)]
 
+    for h in range(2):
+        mm([zb, one], P[4 + h][:], T.one[0:1, :], T.zb[0:1, :], True, False)
     for b in range(4):
-        mm([tcon, one], P[b][:], T.one[0:1, :], T.tcon[0:1, :], True, False)
+        mm([tcon], P[b][:], T.one[0:1, :], T.tcon[0:1, :], True, False)
     vv, cnt, slot = [None] * 4, [None] * 2, [None] * 2
-    for b in range(4):
+
+    def unwrap(b):
         h, odd = b // 2, b % 2
         for j in range(8):
             p = 2 * j + odd
             t = mm([sh, s16], P[b][:, j:512:8], T.sh[:, p:p + 128], T.s16[:, cols(h, 64)], False, j == 7)
-        vv[b] = act([t], T.vv[:, 1024 * h + odd:1024 * h + 1024:2], P[b][:], bias=16.0 * S + 32 + 16 * h)
-    for h in range(2):
-        mm([mks[-1], l1], P[4 + h][:], T.l1[:], T.mk[:, cols(h, 512)], True, False)
-    for h in range(2):
-        cnt[h] = mm([scs[-1], bd], P[4 + h][:], T.bd[:], T.sc[:, cols(h, 512)], False, True)
+        vv[b] = act([t], T.vv[:, 1024 * h + odd:1024 * h + 1024:2], P[b][:], bias=16.0 * S + 12.5 + 16 * h)
+
+    def later(h):
+        for j in range(N):
+            mm([mks[j], l1], P[4 + h][:, j:512:8], T.l1[:], T.mk[:, cols(h, 64, 128 * j)], False, False)
+
+    def through(h):
+        for j in range(N):
+            cnt[h] = mm([scs[j // 4], bd], P[4 + h][:, j:512:8], T.bd[:], T.sc[:, cols(h, 64, 128 * j)], False, j == N - 1)
+
+    unwrap(0)
+    unwrap(1)
+    unwrap(2)
+    later(0)
+    through(0)
+    unwrap(3)
+    later(1)
+    through(1)
     for h in range(2):
         ms = op("v", [cnt[h], d0], lambda e, h=h: e.tensor_tensor_scan(
-            T.ms[:, cols(h, 512)], T.d0[:, cols(h, 512)], P[4 + h][:], 65536.0, OP.min, OP.max))
+            T.ms[:, cols(h, 512)], T.d0[:], P[4 + h][:], 65536.0, OP.min, OP.max))
         slot[h] = ts([ms], T.slot[:, cols(h, 64)], T.ms[:, 512 * h + 7:512 * h + 512:8], float(DUMP), OP.subtract)
     sa = act([slot[0], vv[1], waz], T.wa[:].indirect(T.slot[:, 0:64]), T.vv[:, 0:1024], AF.Silu)
-    sv = cp([slot[1], vv[3], wvz], T.wv[:].indirect(T.slot[:, 64:128]), T.vv[:, 1024:NE])
+    sa = act([slot[1], sa], T.wa[:].indirect(T.slot[:, 64:CUT]), T.vv[:, 1024:16 * CUT], AF.Silu)
+    sv = cp([slot[1], vv[3], wvz], T.wv[:].indirect(T.slot[:, CUT:128]), T.vv[:, 16 * CUT:NE])
 
     lq = [None] * 4
     for q, win, dep, far_side, own_side in (("a", T.wa, sa, T.ra, T.rqa), ("s", T.wv, sv, T.rv, T.rqv)):
@@ -227,7 +251,8 @@ def rank_program(g, core, T, topo):
 
     send([lq[0]], [rq_item(0, far[:hf]), rq_item(1, far[hf:])])
     send([lq[1]], [rq_item(2, far[:hf]), rq_item(3, far[hf:])])
-    send([lq[2]], [rq_item(4, far[:hf]), rq_item(5, far[hf:]), rq_item(6, near)])
+    send([lq[2]], [rq_item(4, far[:hf]), rq_item(5, far[hf:])])
+    send([], [rq_item(6, near)])
     rq_in = [("rq0", 2 * hf), ("rq1", 2 * hf), ("rq2", 2 * hf), ("rq3", len(near))]
 
     gb = cp([geo], T.gb[:], T.gi[:])
@@ -254,160 +279,180 @@ def rank_program(g, core, T, topo):
     omz = fill([], T.om[:, 0:1], 1.0)
     st0 = fill([], T.st[:], 0.0)
     f1 = ts([k1], T.kf[:, 0:1], T.kc[:, 1:2], 48.0, OP.mult)
-    st = fill([st0], T.st[:, 0:256:64], 1.0)
+    st = fill([st0], T.st[:, 0:512:64], 1.0)
     f2 = ts([k3, f1], T.kf[:, 1:2], T.kc[:, 3:4], 6.0, OP.mult, T.kf[:, 0:1], OP.add)
     f3 = ts([k2, f2], T.kf[:, 2:3], T.kc[:, 2:3], T.kf[:, 1:2], OP.add)
     pick = ts([ip, f3], T.pick[:, 0:6], T.ip[:, 0:6], T.kf[:, 2:3], OP.add)
     act([zb], T.ct[:, 0:384], T.zb[:, 0:384])
     ctz = act([zb], T.ct[:, 384:768], T.zb[:, 0:384])
 
-    su, ga, gv, of, col, fa, fv, base, fold, fe = ([None] * 4 for _ in range(10))
+    su, ga, gv, of, col, base, fold, fe = ([None] * 4 for _ in range(8))
+    first = (0, 2, 4, 7, 8)
+    ft = [[] for _ in range(N)]
 
     def place(r):
         return orders(T, topo, r)[0].index(rank)
 
     def f_item(i, engs):
         at = place(serve[i])
-        return (serve[i], engs, "f%d" % (at // 2), [T.fq[:, i, :]], T.fw[:, at, :])
+        return (serve[i], engs, "f%d" % max(at // 2, at - 2), [T.fq[:, i, :]], T.fw[:, at, :])
 
-    def attr(k):
-        c2 = cols(k, 2 * LW)
-        su[k] = ts([rq_in[k], rqo], T.su[:, c2], T.rqi[:, c2], 47.5, OP.subtract, 2.0 ** -5, OP.mult)
-        gv[k] = cp([su[k], att], T.gq[:, cols(2 * k + 1, CAP)], T.aw[:].indirect(T.su[:, cols(2 * k + 1, LW)]))
-        ga[k] = act([su[k], att], T.gq[:, cols(2 * k, CAP)], T.aw[:].indirect(T.su[:, cols(2 * k, LW)]))
+    def splats(k0, k1):
+        c = slice(LW * first[k0], LW * first[k1])
+        x = ts(rq_in[k0:k1 + k1 // 3] + [rqo], T.su[:, c], T.rqi[:, c], 28.0, OP.subtract, 2.0 ** -5, OP.mult)
+        for k in range(k0, k1):
+            su[k] = x
+
+    def attr(k, by_vector):
+        a, b = LW * first[k], LW * first[k + 1]
+        m = a + by_vector
+        if m > a:
+            gv[k] = cp([su[k], att], T.gq[:, 16 * a:16 * m], T.aw[:].indirect(T.su[:, a:m]))
+        ga[k] = act([su[k], att], T.gq[:, 16 * m:16 * b], T.aw[:].indirect(T.su[:, m:b]))
 
     def offsets(k0, k1):
-        c = slice(2 * LW * k0, 2 * LW * k1)
-        vi = cp([rq_in[k] for k in range(k0, k1)] + [rqo], T.vi[:, c], T.rqi[:, c])
-        a = ts([vi], T.t31[:, c], T.vi[:, c], 31, OP.bitwise_and)
-        b = ts([vi], T.t24[:, c], T.vi[:, c], 24, OP.bitwise_and)
-        x = tt([a, b], T.of[:, c], T.t31[:, c], T.t24[:, c], OP.add)
+        c = slice(LW * first[k0], LW * first[k1])
+        magic = 1.5 * 2.0 ** 26
+        ts([], T.r8[:, c], T.rqi[:, c], magic, OP.add, magic, OP.subtract)
+        b = ts([su[k1 - 1]], T.s64[:, c], T.su[:, c], -64.0, OP.mult)
         for k in range(k0, k1):
-            of[k] = x
+            of[k] = b
 
     def lists(k):
-        o = P[6 + k % 2][:, 0:2 * LW]
-        b = 2 * CAP * k
+        a, b = first[k], first[k + 1]
+        o = P[6 + k % 2][:, 0:LW * (b - a)]
+        for n, x in enumerate((T.rqi, T.r8, T.s64)):
+            mm([of[k], idf, col[k - 2] if k > 1 else None], o, T.idf[:], x[:, LW * a:LW * b], n == 0, False)
         for p in range(16):
-            mm([ga[k], gv[k], rb, col[k - 2] if k > 1 else None], o, T.rb[:, 16 - p:144 - p],
-               T.gq[:, b + p:b + 2 * CAP:16], p == 0, False)
-        base[k] = mm([of[k], sb], o, T.sb[:, 0:128], T.of[:, cols(k, 2 * LW)], False, True)
-        for j in range(2):
+            base[k] = mm([ga[k], gv[k], rb], o, T.rb[:, 16 - p:144 - p], T.gq[:, CAP * a + p:CAP * b:16], False, p == 15)
+        for i in range(a, b):
             for h in range(4):
-                fold[k] = mm([fo, ms, fe[k - 2] if k > 1 else None], P[4 + k % 2][:, cols(j, FW)], T.fo[:, 3 - h:131 - h],
-                             T.gq[:, cols(h, FW, b + CAP * j)], h == 0, h == 3, h == 3 and j == 1)
+                fold[k] = mm([fo, ms, fe[k - 2] if k > 1 else None], P[4 + k % 2][:, cols(i - a, FW)], T.fo[:, 3 - h:131 - h],
+                             T.gq[:, cols(h, FW, CAP * i)], h == 0, h == 3, h == 3 and i == b - 1)
 
-    def foot(k):
-        c2 = cols(k, 2 * LW)
-        col[k] = ts([base[k]], T.cu[:, c2], P[6 + k % 2][:, 0:2 * LW], 136.0, OP.add)
-        fv[k] = cp([col[k], dic], T.fq[:, 2 * k + 1, 0:CAP], T.dw[:].indirect(T.cu[:, cols(2 * k + 1, LW)]))
-        fa[k] = act([col[k], dic], T.fq[:, 2 * k, 0:CAP], T.dw[:].indirect(T.cu[:, cols(2 * k, LW)]))
-        fe[k] = act([fold[k]], T.fq[:, 2 * k:2 * k + 2, CAP:RW], P[4 + k % 2][:, 0:2 * FW])
-        if k < 3:
-            send([fv[k], fe[k]], [f_item(2 * k, far[:hf]), f_item(2 * k + 1, far[hf:])])
-        else:
-            send([fe[k]], [f_item(2 * k, near)])
+    def columns(k):
+        a, b = first[k], first[k + 1]
+        col[k] = ts([base[k]], T.cu[:, LW * a:LW * b], P[6 + k % 2][:, 0:LW * (b - a)], 136.0 - 28.5, OP.add)
 
-    attr(0)
+    def folded(k):
+        a, b = first[k], first[k + 1]
+        fe[k] = act([fold[k]], T.fq[:, a:b, CAP:RW], P[4 + k % 2][:, 0:FW * (b - a)])
+
+    def foot(k, i, by, a=0, b=LW):
+        ft[i].append(by([col[k], dic], T.fq[:, i, 16 * a:16 * b], T.dw[:].indirect(T.cu[:, LW * i + a:LW * i + b])))
+
+    def pair(k):
+        columns(k)
+        foot(k, 2 * k + 1, cp)
+        foot(k, 2 * k, act)
+        folded(k)
+        send(ft[2 * k] + ft[2 * k + 1] + [fe[k]], [f_item(2 * k, far[:hf]), f_item(2 * k + 1, far[hf:])])
+
+    def single(k, i):
+        foot(k, i, cp, 0, LW // 2)
+        foot(k, i, act, LW // 2, LW)
+
+    splats(0, 1)
     offsets(0, 1)
+    attr(0, 16)
     lists(0)
-    attr(1)
-    offsets(1, 4)
+    splats(1, 2)
+    offsets(1, 2)
+    attr(1, 10)
+    pair(0)
     lists(1)
-    foot(0)
-    attr(2)
+    splats(2, 4)
+    offsets(2, 4)
+    attr(2, 26)
+    pair(1)
     lists(2)
-    foot(1)
-    attr(3)
+    columns(2)
+    single(2, 4)
+    folded(2)
+    send(ft[4] + [fe[2]], [f_item(4, far)])
+    single(2, 5)
+    send(ft[5], [f_item(5, far)])
+    attr(3, LW // 2)
+    single(2, 6)
+    send(ft[6], [f_item(6, near)])
     lists(3)
-    foot(2)
-    foot(3)
-    f_in = [[("f0", 2 * hf)]] * 2 + [[("f1", 2 * hf)]] * 2 + [[("f2", 2 * hf)]] * 2 + [[("f3", len(near))], [fv[3], fe[3]]]
+    columns(3)
+    folded(3)
+    single(3, 7)
+    f_in = [[("f0", 2 * hf)]] * 2 + [[("f1", 2 * hf)]] * 2 + [[("f2", 2 * hf)], [("f3", 2 * hf)], [("f4", len(near))], ft[7] + [fe[3]]]
 
     al, un = [], []
+
+    def got(i, c):
+        return T.fq[:, i, c] if i == N - 1 else T.fw[:, i, c]
+
     for n, i in enumerate((0, 1, 7, 2, 3, 6, 4, 5)):
-        def got(c, i=i):
-            return T.fq[:, i, c] if i == N - 1 else T.fw[:, i, c]
         for h in range(4):
             a = mm(f_in[i] + [bo, vv[3], al[n - 2] if n > 1 else None], P[n % 2][:, cols(h, FW)], T.bo[:, cols(h, 128)],
-                   got(slice(CAP, RW)), True, True, h == 3)
+                   got(i, slice(CAP, RW)), True, True, h == 3)
         for h in range(4):
             u = mm([un[n - 2] if n > 1 else None], P[2 + n % 2][:, cols(h, FW)], T.sb[:, h:h + 128],
-                   got(slice(CAP, RW)), True, True, h == 3)
-        al.append(tt(f_in[i] + [a], T.al[:, cols(i, CAP, Z)], P[n % 2][:, 0:CAP], got(slice(0, CAP)), OP.mult))
+                   got(i, slice(CAP, RW)), True, True, h == 3)
+        al.append(tt(f_in[i] + [a], T.al[:, cols(i, CAP, Z)], P[n % 2][:, 0:CAP], got(i, slice(0, CAP)), OP.mult))
         un.append(act([u], T.gw[:, cols(i, CAP, Z)], P[2 + n % 2][:, 0:CAP]))
 
-    NC, W = 8, 256
-    om, li, ww, tr, wt, ym, ya = ([None] * NC for _ in range(7))
-    ge, ctp, ct = ([None] * 4 for _ in range(3))
+    plan = {q: [(w[0], int(w[1], 17), int(w[2], 17)) for w in PLAN[q].split()] for q in PLAN}
+    done = {s: [None] * 16 for s in "RLWTKGCXMO"}
     ready = [al[-1], alz, fin]
+    lots = {s: sorted((a, b) for q in "va" for r, a, b in plan[q] if r == s) for s in "KXO"}
+    banks = {"K": (0, 1, 6, 7), "X": (4, 5), "O": (2, 3)}
 
-    def colours(k, by):
-        ge[k] = by([un[-1], gwz, fin], T.ge[:, cols(k, 512)], T.gw[:].indirect(T.fin[:, cols(k, 32)]))
+    def bank(s, x):
+        n = [a <= x < b for a, b in lots[s]].index(True)
+        m = len(banks[s])
+        return P[banks[s][n % m]], x - lots[s][n][0], range(*lots[s][n - m]) if n >= m else ()
 
-    def turn_colours(k):
-        for b in range(4):
-            ctp[k] = mm([selc, ge[k], fe[3], ct[k - 2] if k > 1 else None], P[4 + k % 2][:, cols(b, 24)],
-                        T.ge[:, cols(4 * k + b, 128)], T.selc[:], True, True, b == 3)
+    def needs(s, a, b):
+        blocks = range(a, b)
+        out = [(r, x) for r in {"L": "R", "W": "L", "T": "W", "K": "T", "C": "G", "X": "C", "M": "KX", "O": "M"}.get(s, "")
+               for x in blocks]
+        to = {"T": "K", "C": "X", "M": "O"}.get(s)
+        if to:
+            out += [(to, y) for x in blocks for y in bank(to, x)[2]]
+        return out + ([("R", a - 1)] if s == "L" and a else [])
 
-    def split_colours(k):
-        act([ctp[k], ctz], T.ct[0:64, 192 * k:192 * k + 192:2], P[4 + k % 2][0:64, 0:96])
-        ct[k] = act([], T.ct[64:128, 192 * k + 1:192 * k + 192:2], P[4 + k % 2][64:128, 0:96])
+    def step(q, s, a, b):
+        d = [done[r][x] for r, x in needs(s, a, b)]
+        by = cp if q == "v" else act
+        e, f = slice(128 * a, 128 * b), T.fin[:, 8 * a:8 * b]
+        if s == "R":
+            t = act(ready + [omz], T.om[:, 128 * a + 1:128 * b + 1], T.al[:].indirect(f), scale=-1.0, bias=1.0)
+        elif s == "L":
+            t = op("v", d + [st], lambda v: v.tensor_tensor_scan(T.li[:, e], T.om[:, e], T.st[:, 0:128 * (b - a)], 1.0,
+                                                                OP.mult, OP.max))
+        elif s == "W":
+            t = tt(d + ready, T.ww[:, e], T.al[:].indirect(f), T.li[:, e], OP.mult)
+        elif s == "G":
+            t = by([un[-1], gwz, fin], T.ge[:, e], T.gw[:].indirect(f))
+        elif s == "K":
+            t = by(d, T.wt[:, e], bank(s, a)[0][:, 0:128 * (b - a)])
+        elif s == "X":
+            by(d + [ctz], T.ct[0:64, 48 * a:48 * b:2], bank(s, a)[0][0:64, 0:24 * (b - a)])
+            t = by([], T.ct[64:128, 48 * a + 1:48 * b:2], bank(s, a)[0][64:128, 0:24 * (b - a)])
+        elif s == "O":
+            t = by(d, T.ya[:, 48 * a:48 * b], bank(s, a)[0][:, 0:48 * (b - a)])
+        else:
+            for x in range(a, b):
+                o, at, _ = bank({"T": "K", "C": "X", "M": "O"}[s], x)
+                if s == "T":
+                    t = op("t", d + [idf, col[3]], lambda p, o=o, at=at, x=x: p.transpose(
+                        o[:, cols(at, 128)], T.ww[:, cols(x, 128)], T.idf[:]), x == b - 1)
+                elif s == "C":
+                    t = mm(d + [selc, fe[3]], o[:, cols(at, 24)], T.ge[:, cols(x, 128)], T.selc[:], True, True, x == b - 1)
+                else:
+                    t = mm(d + [un[-1]], o[:, cols(at, 48)], T.wt[:, cols(x, 128)], T.ct[:, cols(x, 48)], True, True, x == b - 1)
+        for x in range(a, b):
+            done[s][x] = t
 
-    def rest(k):
-        om[k] = act(ready + [omz], T.om[:, cols(k, W, 1)], T.al[:].indirect(T.fin[:, cols(k, W // 16)]),
-                    scale=-1.0, bias=1.0)
-
-    def light(k):
-        li[k] = op("v", [om[k], st], lambda e: e.tensor_tensor_scan(
-            T.li[:, cols(k, W)], T.om[:, cols(k, W)], T.st[:], 1.0, OP.mult, OP.max))
-
-    def weight(k):
-        ww[k] = tt(ready + [li[k]], T.ww[:, cols(k, W)], T.al[:].indirect(T.fin[:, cols(k, W // 16)]),
-                   T.li[:, cols(k, W)], OP.mult)
-
-    def turn(k):
-        for h in range(2):
-            tr[k] = op("t", [ww[k], idf, col[3], wt[k - 4] if k > 3 else None], lambda e, h=h: e.transpose(
-                P[(0, 1, 6, 7)[k % 4]][:, cols(h, 128)], T.ww[:, cols(2 * k + h, 128)], T.idf[:]), h == 1)
-
-    def take(k):
-        wt[k] = act([tr[k]], T.wt[:, cols(k, W)], P[(0, 1, 6, 7)[k % 4]][:, 0:W])
-
-    def sums(k):
-        for h in range(2):
-            b = 2 * k + h
-            ym[k] = mm([wt[k], ct[k // 2], un[-1], ya[k - 2] if k > 1 else None], P[2 + k % 2][:, cols(h, 48)],
-                       T.wt[:, cols(b, 128)], T.ct[:, cols(b, 48)], True, True, h == 1)
-
-    def out(k):
-        ya[k] = cp([ym[k]], T.ya[:, cols(k, 96)], P[2 + k % 2][:, 0:96])
-
-    colours(0, cp)
-    for k in range(3):
-        rest(k)
-    turn_colours(0)
-    light(0)
-    for k in range(NC + 3):
-        if k + 1 < NC:
-            light(k + 1)
-        if k < NC:
-            weight(k)
-            turn(k)
-        if 0 <= k - 3 < NC:
-            out(k - 3)
-        if k + 3 < NC:
-            rest(k + 3)
-        if k in (1, 3, 5):
-            colours((k + 1) // 2, cp if k == 3 else act)
-            turn_colours((k + 1) // 2)
-        if k in (1, 3, 5, 7):
-            split_colours(k // 2)
-        if 0 <= k - 1 < NC:
-            take(k - 1)
-        if 0 <= k - 2 < NC:
-            sums(k - 2)
-    yo = cp([ya[NC - 1], pick], T.yo[:], T.ya[:].indirect(T.pick[:, 0:6]))
+    while any(plan.values()):
+        q = [q for q in "vat" if plan[q] and all(done[r][x] for r, x in needs(*plan[q][0]))][0]
+        step(q, *plan[q].pop(0))
+    yo = cp(done["O"] + [pick], T.yo[:], T.ya[:].indirect(T.pick[:, 0:6]))
     y = dma("d_y", [yo], T.y[:], T.yo[:])
 
     wait("s", [y])

@@ -5,15 +5,20 @@ N, S, CAP, NE = 8, 4096, 320, 2048
 LW = CAP // 16
 FW = CAP // 4
 RW = CAP + FW
+SH = 2
+SW = FW + 2 * LW
+PL = 176
+DW = 16 * PL
+LANES = (2, 2, 1, 1, 1, 1)
 Z = 16
 SP = NE // 2 + 128 + CAP
 CUT = 70
 BIG = 8192.0
 DUMP = 8192 - 1280 + 1 - SP
 
-PLAN = {"v": "G04 L02 L24 W02 W24 L48 W46 W68 L8c W8a Lcg Wac Wce Wef X4a K8c Wfg O04 Kef Kfg Oae",
-        "a": "R02 R24 R48 X04 R8c Rcg K04 G4a Gag K48 Xag Kce O4a Oeg",
-        "t": "C04 T02 T24 T46 T68 M04 T8a C4a Tac Tce Tef Cag M8a Tfg M48 Mac Mce Mef Mfg"}
+PLAN = {"v": "G04 L01 L14 W01 W24 L48 W12 W46 W68 L8c Wac Lcg W8a Wce Wef K48 Wfg Kce Kfg Xag Kef O4a Oae Oeg",
+        "a": "R01 R14 R48 R8c Rcg K04 X04 G4a Gag X4a K8c O04",
+        "t": "C04 T01 T24 T12 T46 T68 M04 Tac C4a T8a Tce Tef Cag Tfg M48 M8a Mac Mce Mfg Mef"}
 
 SCRATCH = {
     "ent_s": ("sbuf", [128, 128], "int32"),
@@ -24,8 +29,8 @@ SCRATCH = {
     "tcon": ("sbuf", [128, 512], "bfloat16"), "d0": ("sbuf", [128, 512], "float32"),
     "one": ("sbuf", [128, 128], "bfloat16"), "sh": ("sbuf", [128, 144], "float16"), "sb": ("sbuf", [128, 144], "bfloat16"),
     "idf": ("sbuf", [128, 128], "float32"), "selc": ("sbuf", [128, 24], "bfloat16"),
-    "kc": ("sbuf", [128, 8], "int32"), "kf": ("sbuf", [128, 8], "float32"),
-    "ip": ("sbuf", [128, 8], "int32"), "pick": ("sbuf", [128, 8], "uint16"),
+    "kc": ("sbuf", [128, 256], "float32"),
+    "half": ("sbuf", [128, 2], "float32"), "ip": ("sbuf", [128, 8], "float32"), "pick": ("sbuf", [128, 8], "uint16"),
     "rb": ("sbuf", [128, 144], "bfloat16"), "fo": ("sbuf", [128, 144], "bfloat16"), "bo": ("sbuf", [128, 512], "bfloat16"),
     "ob": ("sbuf", [128, 128], "bfloat16"), "si": ("sbuf", [128, 128], "int32"), "s16": ("sbuf", [128, 128], "float16"),
     "mk": ("sbuf", [128, 1024], "bfloat16"), "sc": ("sbuf", [128, 1024], "bfloat16"), "ms": ("sbuf", [128, 1024], "float32"),
@@ -38,9 +43,12 @@ SCRATCH = {
     "rqa": ("sbuf", [128, LW], "float32"), "rqv": ("sbuf", [128, LW], "float32"), "rqi": ("sbuf", [128, N * LW], "float32"),
     "su": ("sbuf", [128, N * LW], "uint16"), "r8": ("sbuf", [128, N * LW], "float32"),
     "s64": ("sbuf", [128, N * LW], "float32"), "cu": ("sbuf", [128, N * LW], "uint16"),
-    "dw": ("sbuf", [128, S], "bfloat16"), "aw": ("sbuf", [128, S], "bfloat16"),
+    "dw": ("sbuf", [128, DW], "bfloat16"), "aw": ("sbuf", [128, S], "bfloat16"),
     "gi": ("sbuf", [128, 768], "int32"), "gb": ("sbuf", [128, 768], "bfloat16"),
     "gq": ("sbuf", [128, N * CAP], "bfloat16"), "fq": ("sbuf", [128, N, RW], "bfloat16"),
+    "fs": ("sbuf", [128, SH, SW], "bfloat16"), "fx": ("sbuf", [128, SH, SW], "bfloat16"),
+    "dl": ("sbuf", [128, 2, 256], "bfloat16"), "dc": ("dram", [128, DW // 8], "bfloat16"), "dh": ("dram", [128, DW // 8], "bfloat16"),
+    "xw": ("sbuf", [128, SH * DW], "bfloat16"), "cx": ("sbuf", [128, SH * LW], "uint16"),
     "gw": ("sbuf", [128, Z + N * CAP], "bfloat16"), "fw": ("sbuf", [128, N - 1, RW], "bfloat16"),
     "ge": ("sbuf", [128, NE], "bfloat16"), "al": ("sbuf", [128, Z + N * CAP], "float32"),
     "ct": ("sbuf", [128, 768], "float32"), "st": ("sbuf", [128, 512], "bfloat16"),
@@ -52,7 +60,8 @@ for _b in range(8):
     SCRATCH["p%d" % _b] = ("psum", [128, 512], "float32")
 
 SEMAPHORES = ["cv", "ca", "ct", "cg", "d_ent", "d_wa", "d_wv", "d_geo", "d_dic", "d_att", "d_y", "lq0", "lq1", "lq2", "lq3",
-              "sent", "rq0", "rq1", "rq2", "rq3", "f0", "f1", "f2", "f3", "f4"]
+              "sent", "rq0", "rq1", "rq2", "rq3", "f0", "f1", "f2", "f3", "f4", "f5", "f6", "f7",
+              "d_dl", "d_dc", "d_z", "dh", "xw0", "xw1", "xw2", "d_gw"]
 
 
 def orders(T, topo, rank):
@@ -62,15 +71,52 @@ def orders(T, topo, rank):
     j = on[a].index(rank)
     on = [x[j:] + x[:j] for x in on]
     tail = [r for r in on[a] if r != rank] + [rank]
-    ask = [r for k in range(1, len(chips)) for r in on[(a - k) % len(chips)]] + tail
-    serve = [r for k in range(1, len(chips)) for r in on[(a + k) % len(chips)]] + tail
+    ask = [on[(a - k) % len(chips)][x] for x in (1, 0) for k in range(1, len(chips))] + tail
+    serve = [on[(a + k) % len(chips)][x] for x in (1, 0) for k in range(1, len(chips))] + tail
     return ask, serve
+
+
+def helpers(T, topo, rank):
+    c = T.cores[rank]
+    return [h for h in topo.cores_of(c) if topo.die(h) == topo.die(c) and T.rank_of(h) is None]
+
+
+def bits(engs):
+    m = 0
+    for e in engs:
+        m |= 1 << e
+    return m
+
+
+def dictionary_engines(T, topo, rank):
+    far = topo.engines(T.cores[rank], T.cores[orders(T, topo, rank)[1][0]])
+    h = len(far) // SH
+    return [far[h * i:h * i + h] for i in range(SH)]
+
+
+def hand_on(g, core, T, topo):
+    for r in range(N):
+        if core in helpers(T, topo, r)[:SH]:
+            n = helpers(T, topo, r).index(core)
+            owner = orders(T, topo, r)[0][n]
+            landed = len(dictionary_engines(T, topo, owner)[orders(T, topo, owner)[1].index(r)])
+            for q, ks in ((g.sync, range(0, 8, 2)), (g.scalar, range(1, 8, 2))):
+                q.wait_ge(T.sem["dh"], landed)
+                for k in ks:
+                    q.dma_start(T.dw[16 * k:16 * k + 16, :], T.dh[:]).then_inc(T.sem["d_dic"], 16)
+            g.wait_ge(T.sem["d_dic"], 8 * 16)
+            engs = topo.engines(core, T.cores[r])
+            rid, pid, _ = topo.addr(T.cores[r])
+            g.remote_dma_fused([RemoteDMATransfer(dst_ids=[DstId(rid=rid, pnc=pid)], dma_engine_mask=bits(engs),
+                                                  remote_sem=T.sem["xw%d" % n], src=T.dw[:],
+                                                  dst=T.xw[:, DW * n:DW * n + DW])], local_sem=T.sem["sent"])
+            g.wait_ge(T.sem["sent"], len(engs))
 
 
 def rank_program(g, core, T, topo):
     rank = T.rank_of(core)
     if rank is None:
-        return
+        return hand_on(g, core, T, topo)
     ask, serve = orders(T, topo, rank)
     Q = {"v": g.vector, "a": g.scalar, "t": g.tensor, "g": g, "s": g.sync}
     own = {"v": "cv", "a": "ca", "t": "ct", "g": "cg"}
@@ -134,17 +180,11 @@ def rank_program(g, core, T, topo):
     def cols(i, w, at=0):
         return slice(at + w * i, at + w * i + w)
 
-    def bits(engs):
-        m = 0
-        for e in engs:
-            m |= 1 << e
-        return m
-
     def send(deps, items):
         wait("g", deps)
         trs = []
-        for r, engs, s, srcs, dst in items:
-            rid, pid, _ = topo.addr(T.cores[r])
+        for c, engs, s, srcs, dst in items:
+            rid, pid, _ = topo.addr(c)
             trs.append(RemoteDMATransfer(dst_ids=[DstId(rid=rid, pnc=pid)], dma_engine_mask=bits(engs), remote_sem=T.sem[s],
                                          srcs=srcs, dsts=[dst], alu_op=1 if len(srcs) > 1 else 0))
             count["sent"] = count.get("sent", 0) + len(engs)
@@ -160,16 +200,20 @@ def rank_program(g, core, T, topo):
     zb = fill([], T.zb[:], 0.0)
     zh = fill([], T.zh[:], 0.0)
     one = fill([], T.one[:], 1.0)
-    for a in range(3):
-        geo = dma("d_geo", [], T.gi[:, cols(a, 256)], T.geo[a:24:3, :])
+    dl = dma("d_dl", [], T.dl[:], T.dic[:])
     waz = dma("d_wa", [zf], T.wa[0:128:16, SP:SP + N * CAP], T.zf[:])
     wvz = dma("d_wv", [zf], T.wv[0:128:16, SP:SP + N * CAP], T.zf[:])
-    for row, src in ((0, T.opa[:]), (14, T.opa[:]), (2, T.hue[0:24:3, :]), (4, T.hue[1:24:3, :]), (6, T.hue[2:24:3, :])):
+    dma("d_z", [zb], T.fo[:], T.zb[:, 0:144])
+    rb = dma("d_z", [], T.rb[:], T.zb[:, 0:144])
+    dc = dma("d_dc", [dl], T.dc[:], T.dl[:, :, 16:16 + PL])
+    for a in range(3):
+        geo = dma("d_geo", [], T.gi[:, cols(a, 256)], T.geo[a:24:3, :])
+    for row, src in ((0, T.opa[:]), (14, T.opa[:]), (4, T.hue[0:24:3, :]), (8, T.hue[1:24:3, :]), (12, T.hue[2:24:3, :])):
         dma("d_att", [], T.aw[row:128:16, :], src)
     for a in range(4):
         dma("d_att", [], T.aw[32 * a + 1:32 * a + 32:2, :], T.dic[:])
     for k in range(8):
-        dic = dma("d_dic", [], T.dw[cols(k, 16), :], T.dic[:])
+        dic = dma("d_dic", [dc], T.dw[cols(k, 16), :], T.dc[:])
 
     i3 = iota([], T.i3[:], [[-16, 8], [0, 16]], 0, 1)
     tcon = iota([], T.tcon[0:1, :], [[1, 16], [0, 32]], 0, 0, True)
@@ -183,6 +227,13 @@ def rank_program(g, core, T, topo):
     rs = iota([rs], T.rs[:, 0:1024:128], [[-20, 8]], 60, 0, True)
     d0 = act([zb], T.d0[:], T.zb[:], AF.Silu, bias=2 * BIG, scale=0.0)
     d0 = iota([d0], T.d0[:, 0:512:8], [[-16, 64]], DUMP + 16 * 63, 1, True)
+
+    def place(r):
+        return orders(T, topo, r)[0].index(rank)
+
+    def d_item(i):
+        return (helpers(T, topo, serve[i])[place(serve[i])], dictionary_engines(T, topo, rank)[i], "dh", [T.dc[:]], T.dh[:])
+
 
     si = ts([ent], T.si[:], T.ent_s[:], S - 1, OP.bitwise_and)
     ob = ts([ent], T.ob[:], T.ent_s[:], 2.0 ** -12, OP.mult, 135.5 + 2.0 ** -13, OP.add)
@@ -229,172 +280,240 @@ def rank_program(g, core, T, topo):
     sv = cp([slot[1], vv[3], wvz], T.wv[:].indirect(T.slot[:, CUT:128]), T.vv[:, 16 * CUT:NE])
 
     lq = [None] * 4
-    for q, win, dep, far_side, own_side in (("a", T.wa, sa, T.ra, T.rqa), ("s", T.wv, sv, T.rv, T.rqv)):
-        for i in range(N):
-            k = 3 if i == N - 1 else min(i // 2, 2)
-            lq[k] = dma("lq%d" % k, [dep], own_side[:] if k == 3 else far_side[i], win[0:128:16, cols(i, CAP, SP)], q)
+    for q, win, dep, to in (("a", T.wa, sa, T.ra), ("s", T.wv, sv, T.rv)):
+        for i in range(N - 1):
+            k = min(i // 2, 2)
+            lq[k] = dma("lq%d" % k, [dep], to[i], win[0:128:16, cols(i, CAP, SP)], q)
+    gb = cp([geo], T.gb[:], T.gi[:])
+    for a, q in enumerate("sas"):
+        att = dma("d_att", [gb], T.aw[2 + 4 * a:128:16, :], T.gb[:, cols(a, 256)], q)
+    for q, win, to in (("a", T.wa, T.rqa), ("s", T.wv, T.rqv)):
+        lq[3] = dma("lq3", [], to[:], win[0:128:16, cols(N - 1, CAP, SP)], q)
 
-    rb = mark([zb], T.rb[:], T.zb[:, 0:144], [[-16, 9], [1000, 16]], 16 - 8, 256.0)
-    rb = mark([rb], T.rb[:], T.rb[:], [[-16, 9], [1000, 16]], 16 - 10, -1.0)
-    rb = mark([rb], T.rb[:], T.rb[:], [[-16, 9], [1000, 16]], 16 - 12, -16.0)
-    sb = mark([], T.sb[:], T.zb[:, 0:144], [[-1, 144]], 0, 1.0)
-    fo = mark([], T.fo[:], T.zb[:, 0:144], [[-16, 9], [-2, 4], [-1000, 4]], 3000, 1.0)
+    for row, weight in ((2, float(PL)), (6, -1.0), (10, -16.0)):
+        rb = mark([rb], T.rb[:, 16:144:16], T.rb[:, 16:144:16], [[-16, 8]], -row, weight)
+    fo = mark([], T.fo[:, 3:131:4], T.fo[:, 3:131:4], [[-16, 8], [-4, 4]], 0, 1.0)
+    send([dc], [d_item(i) for i in range(SH)])
+    act([sh], T.sb[:], T.sh[:], scale=2.0 ** -5)
+    sb = idf = act([], T.idf[:], T.sh[:, 0:128], scale=2.0 ** -5)
+    iota([], T.kc[0:1, 0:128], [[6, 8], [48, 8], [1, 2]], 0, 0, True)
+    kc = act([], T.kc[0:1, 128:256], T.one[0:1, :])
+    ip = iota([], T.ip[0:1, 0:6], [[2, 3], [384, 2]], 0, 0, True)
     bo = mark([], T.bo[:], T.zb[:], [[-1, 4], [-16, 8], [0, 16]], 0, 1.0)
-    idf = mark([zf], T.idf[:], T.zf[:, 0:128], [[-1, 128]], 0, 1.0)
-    selc = mark([], T.selc[:], T.zb[:, 0:24], [[-16, 8], [-4, 3]], -4, 1.0)
-    kc = iota([], T.kc[:, 0:1], [[0, 1]], 0, 1)
-    ip = iota([], T.ip[:, 0:6], [[2, 3], [384, 2]], 0, 0)
 
     def rq_item(i, engs):
         at = orders(T, topo, ask[i])[1].index(rank)
-        return (ask[i], engs, "rq%d" % (at // 2), [T.ra[i], T.rv[i]], T.rqi[:, cols(at, LW)])
+        return (T.cores[ask[i]], engs, "rq%d" % (at // 2), [T.ra[i], T.rv[i]], T.rqi[:, cols(at, LW)])
 
     send([lq[0]], [rq_item(0, far[:hf]), rq_item(1, far[hf:])])
     send([lq[1]], [rq_item(2, far[:hf]), rq_item(3, far[hf:])])
     send([lq[2]], [rq_item(4, far[:hf]), rq_item(5, far[hf:])])
     send([], [rq_item(6, near)])
+    selc = mark([], T.selc[:], T.zb[:, 0:24], [[-16, 8], [-4, 3]], -4, 1.0)
     rq_in = [("rq0", 2 * hf), ("rq1", 2 * hf), ("rq2", 2 * hf), ("rq3", len(near))]
 
-    gb = cp([geo], T.gb[:], T.gi[:])
-    for a in range(3):
-        att = dma("d_att", [gb], T.aw[8 + 2 * a:128:16, :], T.gb[:, cols(a, 256)])
 
     at0 = float(DUMP + SP)
     m7 = T.ms[:, 7:1024:8]
     xd = ts([], T.xd[:], m7, at0 + 9.5, OP.subtract, 0.05, OP.mult)
-    xa = ts([], T.xa[:], m7, at0 - Z // 16, OP.subtract, 16.0, OP.mult)
-    xp = ts([xd], T.xp[:], T.xd[:], 15, OP.bitwise_and)
-    xb = ts([xd], T.xb[:], T.xd[:], -300.0, OP.mult)
-    xc = ts([xp], T.xc[:], T.xp[:], -19.0, OP.mult)
-    xa = tt([xa, xb], T.xa[:], T.xa[:], T.xb[:], OP.add)
-    k1 = ts([kc], T.kc[:, 1:2], T.kc[:, 0:1], 15, OP.bitwise_and, 1, OP.arith_shift_right)
-    xa = tt([xa, xc], T.xa[:], T.xa[:], T.xc[:], OP.add)
-    k2 = ts([kc], T.kc[:, 2:3], T.kc[:, 0:1], 1, OP.bitwise_and)
-    fin = cp([xa], T.fin[:], T.xa[:])
+    xa = act([ms], T.xa[:], m7, scale=16.0, bias=Z - 16 * at0)
+    xp = ts([xd], T.xp[:], T.xd[:], 4, OP.arith_shift_right)
+    xb = ts([xd], T.xb[:], T.xd[:], -319.0, OP.mult)
+    xc = ts([xp], T.xc[:], T.xp[:], 304.0, OP.mult)
+    for n, x in enumerate((T.xa, T.xb, T.xc)):
+        t = mm([xa, xc, idf, vv[3]], P[0][:, 0:128], T.idf[:], x[:], n == 0, n == 2)
+    mm([kc, ip], P[1][:, 0:6], T.kc[0:1, 0:128], T.kc[0:1, 128:134], True, False)
+    pick = mm([], P[1][:, 0:6], T.kc[0:1, 128:256], T.ip[0:1, 0:6], False, True)
+    fin = t
+    st = act([], T.st[:], T.zb[:])
+    gwz = act([], T.gw[:, 0:Z], T.zb[:, 0:Z])
+    alz = act([], T.al[:, 0:Z], T.zb[:, 0:Z])
+    omz = act([], T.om[:, 0:1], T.one[:, 0:1])
+    st = act([st], T.st[:, 0:512:64], T.one[:, 0:8])
     rqo = tt([lq[3]], T.rqi[:, cols(N - 1, LW)], T.rqa[:], T.rqv[:], OP.add)
+    half = mark([], T.half[:], T.zf[:, 0:2], [[0, 2]], 1, 0.0)
+    half = op("g", [half], lambda e: e.affine_select(T.half[:, 0:1], T.half[:, 0:1], [[0, 1]], OP.is_ge, 1.0, -64, 1))
+    half = op("g", [half], lambda e: e.affine_select(T.half[:, 1:2], T.half[:, 1:2], [[0, 1]], OP.is_gt, 1.0, 64, -1))
 
-    k3 = ts([kc], T.kc[:, 3:4], T.kc[:, 0:1], 4, OP.arith_shift_right)
-    gwz = fill([], T.gw[:, 0:Z], 0.0)
-    alz = fill([], T.al[:, 0:Z], 0.0)
-    omz = fill([], T.om[:, 0:1], 1.0)
-    st0 = fill([], T.st[:], 0.0)
-    f1 = ts([k1], T.kf[:, 0:1], T.kc[:, 1:2], 48.0, OP.mult)
-    st = fill([st0], T.st[:, 0:512:64], 1.0)
-    f2 = ts([k3, f1], T.kf[:, 1:2], T.kc[:, 3:4], 6.0, OP.mult, T.kf[:, 0:1], OP.add)
-    f3 = ts([k2, f2], T.kf[:, 2:3], T.kc[:, 2:3], T.kf[:, 1:2], OP.add)
-    pick = ts([ip, f3], T.pick[:, 0:6], T.ip[:, 0:6], T.kf[:, 2:3], OP.add)
-    act([zb], T.ct[:, 0:384], T.zb[:, 0:384])
-    ctz = act([zb], T.ct[:, 384:768], T.zb[:, 0:384])
+    su, of, col, base, fold, fe = ([None] * N for _ in range(6))
+    ga, ft = [[] for _ in range(N)], [[] for _ in range(N)]
+    lot, folds_lot = [], []
 
-    su, ga, gv, of, col, base, fold, fe = ([None] * 4 for _ in range(8))
-    first = (0, 2, 4, 7, 8)
-    ft = [[] for _ in range(N)]
+    def mark_all(x, a, b, t):
+        for i in range(a, b):
+            x[i] = t
 
-    def place(r):
-        return orders(T, topo, r)[0].index(rank)
-
-    def f_item(i, engs):
-        at = place(serve[i])
-        return (serve[i], engs, "f%d" % max(at // 2, at - 2), [T.fq[:, i, :]], T.fw[:, at, :])
-
-    def splats(k0, k1):
-        c = slice(LW * first[k0], LW * first[k1])
-        x = ts(rq_in[k0:k1 + k1 // 3] + [rqo], T.su[:, c], T.rqi[:, c], 28.0, OP.subtract, 2.0 ** -5, OP.mult)
-        for k in range(k0, k1):
-            su[k] = x
-
-    def attr(k, by_vector):
-        a, b = LW * first[k], LW * first[k + 1]
-        m = a + by_vector
-        if m > a:
-            gv[k] = cp([su[k], att], T.gq[:, 16 * a:16 * m], T.aw[:].indirect(T.su[:, a:m]))
-        ga[k] = act([su[k], att], T.gq[:, 16 * m:16 * b], T.aw[:].indirect(T.su[:, m:b]))
-
-    def offsets(k0, k1):
-        c = slice(LW * first[k0], LW * first[k1])
+    def splats(a, b):
+        c = slice(LW * a, LW * b)
         magic = 1.5 * 2.0 ** 26
+        x = ts([rq_in[i // 2] if i < N - 1 else rqo for i in range(a, b)], T.su[:, c], T.rqi[:, c], 28.0, OP.subtract,
+               2.0 ** -5, OP.mult)
+        mark_all(su, a, b, x)
         ts([], T.r8[:, c], T.rqi[:, c], magic, OP.add, magic, OP.subtract)
-        b = ts([su[k1 - 1]], T.s64[:, c], T.su[:, c], -64.0, OP.mult)
-        for k in range(k0, k1):
-            of[k] = b
+        mark_all(of, a, b, ts([x], T.s64[:, c], T.su[:, c], -64.0, OP.mult, 120 - 28.5, OP.add))
 
-    def lists(k):
-        a, b = first[k], first[k + 1]
-        o = P[6 + k % 2][:, 0:LW * (b - a)]
-        for n, x in enumerate((T.rqi, T.r8, T.s64)):
-            mm([of[k], idf, col[k - 2] if k > 1 else None], o, T.idf[:], x[:, LW * a:LW * b], n == 0, False)
+    def rows(x, y, step=1):
+        return T.gq[:, x:y:step] if x < CAP * (N - 1) else T.gw[:, Z + x:Z + y:step]
+
+    def attr(a, b, by_vector):
+        m = LW * a + by_vector
+        for by, x, y in ((cp, LW * a, m), (act, m, LW * b)):
+            if y > x:
+                t = by(su[a:b] + [att], rows(16 * x, 16 * y), T.aw[:].indirect(T.su[:, x:y]))
+                for i in range(a, b):
+                    ga[i].append(t)
+
+    def tiles(a, b):
+        k = len(lot)
+        lot.append((a, b))
+        for n, x in enumerate((T.s64, T.rqi, T.r8)):
+            mm(of[a:b] + [idf] + (col[slice(*lot[k - 2])] if k > 1 else []), P[6 + k % 2][:, 0:LW * (b - a)], T.idf[:],
+               x[:, LW * a:LW * b], n == 0, False)
+
+    def lists(a, b):
         for p in range(16):
-            base[k] = mm([ga[k], gv[k], rb], o, T.rb[:, 16 - p:144 - p], T.gq[:, CAP * a + p:CAP * b:16], False, p == 15)
+            base[a] = mm(sum(ga[a:b], []) + [rb], P[6 + lot.index((a, b)) % 2][:, 0:LW * (b - a)], T.rb[:, 16 - p:144 - p],
+                         rows(CAP * a + p, CAP * b, 16), False, p == 15)
+
+    def folds(a, b):
+        k = len(folds_lot)
+        folds_lot.append((a, b))
+        lot = folds_lot
         for i in range(a, b):
             for h in range(4):
-                fold[k] = mm([fo, ms, fe[k - 2] if k > 1 else None], P[4 + k % 2][:, cols(i - a, FW)], T.fo[:, 3 - h:131 - h],
-                             T.gq[:, cols(h, FW, CAP * i)], h == 0, h == 3, h == 3 and i == b - 1)
+                fold[a] = mm(ga[i] + [fo, ms, fe[lot[k - 2][0]] if k > 1 else None], P[4 + k % 2][:, cols(i - a, FW)],
+                             T.fo[:, 3 - h:131 - h], T.gq[:, cols(h, FW, CAP * i)], h == 0, h == 3, h == 3 and i == b - 1)
 
-    def columns(k):
-        a, b = first[k], first[k + 1]
-        col[k] = ts([base[k]], T.cu[:, LW * a:LW * b], P[6 + k % 2][:, 0:LW * (b - a)], 136.0 - 28.5, OP.add)
+    def columns(a, b):
+        k = [x <= a < y for x, y in lot].index(True)
+        first = lot[k][0]
+        o = P[6 + k % 2][:, LW * (a - first):LW * (b - first)]
+        if a >= SH:
+            return mark_all(col, a, b, cp([base[first]], T.cu[:, LW * a:LW * b], o))
+        magic = 1.5 * 2.0 ** 28
+        hi = ts([base[first]], T.fs[:, a:b, FW:FW + LW], o, magic, OP.add, magic, OP.subtract)
+        mark_all(col, a, b, tt([hi], T.fs[:, a:b, FW + LW:SW], o, T.fs[:, a:b, FW:FW + LW], OP.subtract))
 
-    def folded(k):
-        a, b = first[k], first[k + 1]
-        fe[k] = act([fold[k]], T.fq[:, a:b, CAP:RW], P[4 + k % 2][:, 0:FW * (b - a)])
+    def folded(a, b):
+        out = T.fs[:, a:b, 0:FW] if a < SH else T.fq[:, a:b, CAP:RW]
+        mark_all(fe, a, b, act([fold[a]], out, P[4 + folds_lot.index((a, b)) % 2][:, 0:FW * (b - a)]))
 
-    def foot(k, i, by, a=0, b=LW):
-        ft[i].append(by([col[k], dic], T.fq[:, i, 16 * a:16 * b], T.dw[:].indirect(T.cu[:, LW * i + a:LW * i + b])))
+    def foot(i, by_vector=LW // 2):
+        for by, a, b in ((cp, 0, by_vector), (act, by_vector, LW)):
+            if b > a and i >= SH:
+                ft[i].append(by([col[i], dic], T.fq[:, i, 16 * a:16 * b], T.dw[:].indirect(T.cu[:, LW * i + a:LW * i + b])))
+            elif b > a:
+                ft[i].append(by([cx[i], ("xw%d" % i, len(far + near))], T.fw[:, i, 16 * a:16 * b],
+                                T.xw[:, cols(i, DW)].indirect(T.cx[:, LW * i + a:LW * i + b])))
 
-    def pair(k):
-        columns(k)
-        foot(k, 2 * k + 1, cp)
-        foot(k, 2 * k, act)
-        folded(k)
-        send(ft[2 * k] + ft[2 * k + 1] + [fe[k]], [f_item(2 * k, far[:hf]), f_item(2 * k + 1, far[hf:])])
+    def answer(*items):
+        out = []
+        for i, engs in items:
+            at = place(serve[i])
+            src, dst = (T.fs[:, i, :], T.fx[:, at, :]) if i < SH else (T.fq[:, i, :], T.fw[:, at, :])
+            out.append((T.cores[serve[i]], engs, "f%d" % at, [src], dst))
+        send([t for i, _ in items for t in ft[i] + [fe[i], col[i]]], out)
 
-    def single(k, i):
-        foot(k, i, cp, 0, LW // 2)
-        foot(k, i, act, LW // 2, LW)
+    def answer_neighbour(footprints):
+        i = N - 2
+        if footprints:
+            return send(ft[i], [(T.cores[serve[i]], near, "f7", [T.fq[:, i, 0:CAP]], T.fw[:, i, 0:CAP])])
+        send(ga[i], [(T.cores[serve[i]], near, "f6", [rows(CAP * i, CAP * i + CAP)], T.gw[:, cols(i, CAP, Z)])])
 
-    splats(0, 1)
-    offsets(0, 1)
-    attr(0, 16)
-    lists(0)
-    splats(1, 2)
-    offsets(1, 2)
-    attr(1, 10)
-    pair(0)
-    lists(1)
+    landed = [("f%d" % i, len(far) // LANES[i]) for i in range(N - 2)] + [("f6", len(near))]
+    al, un, und, theirs, cx = [], [], [], [], [None] * SH
+
+    def folded_of(i):
+        if i >= N - 2:
+            return T.gw[:, cols(i, CAP, Z)], ga[i] if i == N - 1 else [landed[i]]
+        return T.fx[:, i, 0:FW] if i < SH else T.fw[:, i, CAP:RW], [landed[i]]
+
+    def alpha(i):
+        f, d = folded_of(i)
+        n = len(al)
+        parts, w = (4, FW) if i < N - 2 else (1, CAP)
+        for h in range(parts):
+            a = mm(d + [bo, pick, al[n - 2] if n > 1 else None], P[n % 2][:, cols(h, w)], T.bo[:, cols(h, 128)], f,
+                   True, True, h == parts - 1)
+        mine = ft[i] if i < SH or i == N - 1 else [("f7", len(near))] if i == N - 2 else [landed[i]]
+        al.append(tt(d + mine + [a], T.al[:, cols(i, CAP, Z)], P[n % 2][:, 0:CAP],
+                     T.fq[:, i, 0:CAP] if i == N - 1 else T.fw[:, i, 0:CAP], OP.mult))
+
+    def hues(i, by=act):
+        f, d = folded_of(i)
+        m = len(un)
+        for h in range(4):
+            u = mm(d + [vv[3], un[m - 2] if m > 1 else None], P[2 + m % 2][:, cols(h, FW)], T.sb[:, h:h + 128], f,
+                   True, True, h == 3)
+        un.append(by([u], T.gw[:, cols(i, CAP, Z)], P[2 + m % 2][:, 0:CAP]))
+
+    def their_columns(a, b):
+        o = P[6 + len(lot) % 2]
+        for i in range(a, b):
+            mm([landed[i], sb] + col, o[:, cols(i, LW)], T.sb[:, 0:128], T.fx[:, i, FW:FW + LW], True, False)
+            t = mm([], o[:, cols(i, LW)], T.sb[:, 0:128], T.fx[:, i, FW + LW:SW], False, True)
+        theirs.append(cp([t], T.cx[:, LW * a:LW * b], o[:, LW * a:LW * b]))
+        mark_all(cx, a, b, theirs[-1])
+
+    splats(7, 8)
+    attr(7, 8, 0)
+    fin = cp([fin], T.fin[:], P[0][:, 0:128])
+    pick = cp([pick], T.pick[:, 0:6], P[1][:, 0:6])
+    tiles(7, 8)
+    lists(7, 8)
+    splats(0, 2)
+    attr(0, 2, 16)
     splats(2, 4)
-    offsets(2, 4)
-    attr(2, 26)
-    pair(1)
-    lists(2)
-    columns(2)
-    single(2, 4)
-    folded(2)
-    send(ft[4] + [fe[2]], [f_item(4, far)])
-    single(2, 5)
-    send(ft[5], [f_item(5, far)])
-    attr(3, LW // 2)
-    single(2, 6)
-    send(ft[6], [f_item(6, near)])
-    lists(3)
-    columns(3)
-    folded(3)
-    single(3, 7)
-    f_in = [[("f0", 2 * hf)]] * 2 + [[("f1", 2 * hf)]] * 2 + [[("f2", 2 * hf)], [("f3", 2 * hf)], [("f4", len(near))], ft[7] + [fe[3]]]
+    attr(2, 4, 8)
+    tiles(0, 2)
+    lists(0, 2)
+    folds(0, 2)
+    columns(7, 8)
+    columns(0, 2)
+    folded(0, 2)
+    answer((0, far[:hf]), (1, far[hf:]))
+    tiles(2, 4)
+    splats(4, 7)
+    lists(2, 4)
+    attr(4, 7, 22)
+    answer_neighbour(False)
+    folds(2, 4)
+    tiles(4, 7)
+    columns(2, 4)
+    lists(4, 7)
+    foot(2, 18)
+    folded(2, 4)
+    answer((2, far))
+    foot(3, 2)
+    answer((3, far))
+    folds(4, 6)
+    columns(4, 7)
+    folded(4, 6)
+    foot(4, LW)
+    answer((4, far))
+    foot(6, 0)
+    answer_neighbour(True)
+    foot(5, 16)
+    answer((5, far))
 
-    al, un = [], []
-
-    def got(i, c):
-        return T.fq[:, i, c] if i == N - 1 else T.fw[:, i, c]
-
-    for n, i in enumerate((0, 1, 7, 2, 3, 6, 4, 5)):
-        for h in range(4):
-            a = mm(f_in[i] + [bo, vv[3], al[n - 2] if n > 1 else None], P[n % 2][:, cols(h, FW)], T.bo[:, cols(h, 128)],
-                   got(i, slice(CAP, RW)), True, True, h == 3)
-        for h in range(4):
-            u = mm([un[n - 2] if n > 1 else None], P[2 + n % 2][:, cols(h, FW)], T.sb[:, h:h + 128],
-                   got(i, slice(CAP, RW)), True, True, h == 3)
-        al.append(tt(f_in[i] + [a], T.al[:, cols(i, CAP, Z)], P[n % 2][:, 0:CAP], got(i, slice(0, CAP)), OP.mult))
-        un.append(act([u], T.gw[:, cols(i, CAP, Z)], P[2 + n % 2][:, 0:CAP]))
+    foot(7, 12)
+    hues(1)
+    their_columns(0, 2)
+    alpha(7)
+    foot(0, 4)
+    alpha(0)
+    alpha(2)
+    foot(1, 0)
+    hues(0)
+    alpha(1)
+    hues(2)
+    alpha(3)
+    hues(3)
+    alpha(6)
+    hues(4)
+    alpha(4)
+    hues(5)
+    alpha(5)
 
     plan = {q: [(w[0], int(w[1], 17), int(w[2], 17)) for w in PLAN[q].split()] for q in PLAN}
     done = {s: [None] * 16 for s in "RLWTKGCXMO"}
@@ -428,24 +547,25 @@ def rank_program(g, core, T, topo):
         elif s == "W":
             t = tt(d + ready, T.ww[:, e], T.al[:].indirect(f), T.li[:, e], OP.mult)
         elif s == "G":
-            t = by([un[-1], gwz, fin], T.ge[:, e], T.gw[:].indirect(f))
+            t = by(un + ga[N - 1] + [landed[N - 2], gwz, fin], T.ge[:, e], T.gw[:].indirect(f))
         elif s == "K":
             t = by(d, T.wt[:, e], bank(s, a)[0][:, 0:128 * (b - a)])
         elif s == "X":
-            by(d + [ctz], T.ct[0:64, 48 * a:48 * b:2], bank(s, a)[0][0:64, 0:24 * (b - a)])
-            t = by([], T.ct[64:128, 48 * a + 1:48 * b:2], bank(s, a)[0][64:128, 0:24 * (b - a)])
+            for h in range(2):
+                o, x, m = T.ct[:, 48 * a + h:48 * b:2], bank(s, a)[0][:, 0:24 * (b - a)], T.half[:, h:h + 1]
+                t = ts(d + [half], o, x, m, OP.mult) if q == "v" else act(d + [half], o, x, scale=m)
         elif s == "O":
             t = by(d, T.ya[:, 48 * a:48 * b], bank(s, a)[0][:, 0:48 * (b - a)])
         else:
             for x in range(a, b):
                 o, at, _ = bank({"T": "K", "C": "X", "M": "O"}[s], x)
                 if s == "T":
-                    t = op("t", d + [idf, col[3]], lambda p, o=o, at=at, x=x: p.transpose(
+                    t = op("t", d + [idf] + theirs, lambda p, o=o, at=at, x=x: p.transpose(
                         o[:, cols(at, 128)], T.ww[:, cols(x, 128)], T.idf[:]), x == b - 1)
                 elif s == "C":
-                    t = mm(d + [selc, fe[3]], o[:, cols(at, 24)], T.ge[:, cols(x, 128)], T.selc[:], True, True, x == b - 1)
+                    t = mm(d + [selc] + fe, o[:, cols(at, 24)], T.ge[:, cols(x, 128)], T.selc[:], True, True, x == b - 1)
                 else:
-                    t = mm(d + [un[-1]], o[:, cols(at, 48)], T.wt[:, cols(x, 128)], T.ct[:, cols(x, 48)], True, True, x == b - 1)
+                    t = mm(d + un, o[:, cols(at, 48)], T.wt[:, cols(x, 128)], T.ct[:, cols(x, 48)], True, True, x == b - 1)
         for x in range(a, b):
             done[s][x] = t
 

from concourse.bass import DstId, RemoteDMATransfer
from concourse.mybir import AluOpType as OP, ActivationFunctionType as AF

N, S, CAP, NE = 8, 4096, 320, 2048
LW = CAP // 16
FW = CAP // 4
RW = CAP + FW
SH = 2
SW = FW + 2 * LW
PL = 176
DW = 16 * PL
LANES = (2, 2, 1, 1, 1, 1)
Z = 16
SP = NE // 2 + 128 + CAP
CUT = 70
BIG = 8192.0
DUMP = 8192 - 1280 + 1 - SP

PLAN = {"v": "G04 L01 L14 W01 W24 L48 W12 W46 W68 L8c Wac Lcg W8a Wce Wef K48 Wfg Kce Kfg Xag Kef O4a Oae Oeg",
        "a": "R01 R14 R48 R8c Rcg K04 X04 G4a Gag X4a K8c O04",
        "t": "C04 T01 T24 T12 T46 T68 M04 Tac C4a T8a Tce Tef Cag Tfg M48 M8a Mac Mce Mfg Mef"}

SCRATCH = {
    "ent_s": ("sbuf", [128, 128], "int32"),
    "zf": ("sbuf", [128, 160], "float32"), "zb": ("sbuf", [128, 512], "bfloat16"), "zh": ("sbuf", [128, 144], "float16"),
    "i3": ("sbuf", [128, 128], "int32"), "i3s": ("sbuf", [128, 128], "int32"),
    "bd": ("sbuf", [128, 128], "bfloat16"), "nbd": ("sbuf", [128, 128], "bfloat16"),
    "l0": ("sbuf", [128, 128], "bfloat16"), "l1": ("sbuf", [128, 128], "bfloat16"),
    "tcon": ("sbuf", [128, 512], "bfloat16"), "d0": ("sbuf", [128, 512], "float32"),
    "one": ("sbuf", [128, 128], "bfloat16"), "sh": ("sbuf", [128, 144], "float16"), "sb": ("sbuf", [128, 144], "bfloat16"),
    "idf": ("sbuf", [128, 128], "float32"), "selc": ("sbuf", [128, 24], "bfloat16"),
    "kc": ("sbuf", [128, 256], "float32"),
    "half": ("sbuf", [128, 2], "float32"), "ip": ("sbuf", [128, 8], "float32"), "pick": ("sbuf", [128, 8], "uint16"),
    "rb": ("sbuf", [128, 144], "bfloat16"), "fo": ("sbuf", [128, 144], "bfloat16"), "bo": ("sbuf", [128, 512], "bfloat16"),
    "ob": ("sbuf", [128, 128], "bfloat16"), "si": ("sbuf", [128, 128], "int32"), "s16": ("sbuf", [128, 128], "float16"),
    "mk": ("sbuf", [128, 1024], "bfloat16"), "sc": ("sbuf", [128, 1024], "bfloat16"), "ms": ("sbuf", [128, 1024], "float32"),
    "rs": ("sbuf", [128, 1024], "bfloat16"), "slot": ("sbuf", [128, 128], "uint16"), "fin": ("sbuf", [128, 128], "uint16"),
    "xd": ("sbuf", [128, 128], "int32"), "xp": ("sbuf", [128, 128], "int32"),
    "xa": ("sbuf", [128, 128], "float32"), "xb": ("sbuf", [128, 128], "float32"), "xc": ("sbuf", [128, 128], "float32"),
    "vv": ("sbuf", [128, NE], "float32"),
    "wa": ("sbuf", [128, SP + N * CAP], "float32"), "wv": ("sbuf", [128, SP + N * CAP], "float32"),
    "ra": ("dram", [N - 1, 128, LW], "float32"), "rv": ("dram", [N - 1, 128, LW], "float32"),
    "rqa": ("sbuf", [128, LW], "float32"), "rqv": ("sbuf", [128, LW], "float32"), "rqi": ("sbuf", [128, N * LW], "float32"),
    "su": ("sbuf", [128, N * LW], "uint16"), "r8": ("sbuf", [128, N * LW], "float32"),
    "s64": ("sbuf", [128, N * LW], "float32"), "cu": ("sbuf", [128, N * LW], "uint16"),
    "dw": ("sbuf", [128, DW], "bfloat16"), "aw": ("sbuf", [128, S], "bfloat16"),
    "gi": ("sbuf", [128, 768], "int32"), "gb": ("sbuf", [128, 768], "bfloat16"),
    "gq": ("sbuf", [128, N * CAP], "bfloat16"), "fq": ("sbuf", [128, N, RW], "bfloat16"),
    "fs": ("sbuf", [128, SH, SW], "bfloat16"), "fx": ("sbuf", [128, SH, SW], "bfloat16"),
    "dl": ("sbuf", [128, 2, 256], "bfloat16"), "dc": ("dram", [128, DW // 8], "bfloat16"), "dh": ("dram", [128, DW // 8], "bfloat16"),
    "xw": ("sbuf", [128, SH * DW], "bfloat16"), "cx": ("sbuf", [128, SH * LW], "uint16"),
    "gw": ("sbuf", [128, Z + N * CAP], "bfloat16"), "fw": ("sbuf", [128, N - 1, RW], "bfloat16"),
    "ge": ("sbuf", [128, NE], "bfloat16"), "al": ("sbuf", [128, Z + N * CAP], "float32"),
    "ct": ("sbuf", [128, 768], "float32"), "st": ("sbuf", [128, 512], "bfloat16"),
    "om": ("sbuf", [128, NE + 4], "float32"), "li": ("sbuf", [128, NE], "float32"),
    "ww": ("sbuf", [128, NE], "float32"), "wt": ("sbuf", [128, NE], "float32"),
    "ya": ("sbuf", [128, 768], "float32"), "yo": ("sbuf", [128, 96], "float32"),
}
for _b in range(8):
    SCRATCH["p%d" % _b] = ("psum", [128, 512], "float32")

SEMAPHORES = ["cv", "ca", "ct", "cg", "d_ent", "d_wa", "d_wv", "d_geo", "d_dic", "d_att", "d_y", "lq0", "lq1", "lq2", "lq3",
              "sent", "rq0", "rq1", "rq2", "rq3", "f0", "f1", "f2", "f3", "f4", "f5", "f6", "f7",
              "d_dl", "d_dc", "d_z", "dh", "xw0", "xw1", "xw2", "d_gw"]


def orders(T, topo, rank):
    chips = sorted(set(topo.chip(c) for c in T.cores))
    on = [[r for r in range(N) if topo.chip(T.cores[r]) == ch] for ch in chips]
    a = chips.index(topo.chip(T.cores[rank]))
    j = on[a].index(rank)
    on = [x[j:] + x[:j] for x in on]
    tail = [r for r in on[a] if r != rank] + [rank]
    ask = [on[(a - k) % len(chips)][x] for x in (1, 0) for k in range(1, len(chips))] + tail
    serve = [on[(a + k) % len(chips)][x] for x in (1, 0) for k in range(1, len(chips))] + tail
    return ask, serve


def helpers(T, topo, rank):
    c = T.cores[rank]
    return [h for h in topo.cores_of(c) if topo.die(h) == topo.die(c) and T.rank_of(h) is None]


def bits(engs):
    m = 0
    for e in engs:
        m |= 1 << e
    return m


def dictionary_engines(T, topo, rank):
    far = topo.engines(T.cores[rank], T.cores[orders(T, topo, rank)[1][0]])
    h = len(far) // SH
    return [far[h * i:h * i + h] for i in range(SH)]


def hand_on(g, core, T, topo):
    for r in range(N):
        if core in helpers(T, topo, r)[:SH]:
            n = helpers(T, topo, r).index(core)
            owner = orders(T, topo, r)[0][n]
            landed = len(dictionary_engines(T, topo, owner)[orders(T, topo, owner)[1].index(r)])
            for q, ks in ((g.sync, range(0, 8, 2)), (g.scalar, range(1, 8, 2))):
                q.wait_ge(T.sem["dh"], landed)
                for k in ks:
                    q.dma_start(T.dw[16 * k:16 * k + 16, :], T.dh[:]).then_inc(T.sem["d_dic"], 16)
            g.wait_ge(T.sem["d_dic"], 8 * 16)
            engs = topo.engines(core, T.cores[r])
            rid, pid, _ = topo.addr(T.cores[r])
            g.remote_dma_fused([RemoteDMATransfer(dst_ids=[DstId(rid=rid, pnc=pid)], dma_engine_mask=bits(engs),
                                                  remote_sem=T.sem["xw%d" % n], src=T.dw[:],
                                                  dst=T.xw[:, DW * n:DW * n + DW])], local_sem=T.sem["sent"])
            g.wait_ge(T.sem["sent"], len(engs))


def rank_program(g, core, T, topo):
    rank = T.rank_of(core)
    if rank is None:
        return hand_on(g, core, T, topo)
    ask, serve = orders(T, topo, rank)
    Q = {"v": g.vector, "a": g.scalar, "t": g.tensor, "g": g, "s": g.sync}
    own = {"v": "cv", "a": "ca", "t": "ct", "g": "cg"}
    count, seen = {}, {}

    def wait(q, deps):
        need = {}
        for d in deps:
            if d is not None and d[1] > need.get(d[0], 0):
                need[d[0]] = d[1]
        for s, v in need.items():
            if seen.get((q, s), 0) < v:
                Q[q].wait_ge(T.sem[s], v)
                seen[(q, s)] = v

    def op(q, deps, make, mark=True):
        wait(q, deps)
        ins = make(Q[q])
        if not mark:
            return None
        s = own[q]
        count[s] = count.get(s, 0) + 1
        ins.then_inc(T.sem[s], 1)
        return (s, count[s])

    def dma(s, deps, out, in_, q="s"):
        wait(q, deps)
        Q[q].dma_start(out, in_).then_inc(T.sem[s], 16)
        count[s] = count.get(s, 0) + 16
        return (s, count[s])

    def ts(deps, out, in0, s1, o0, s2=None, o1=None):
        if o1 is None:
            return op("v", deps, lambda e: e.tensor_scalar(out, in0, s1, None, o0))
        return op("v", deps, lambda e: e.tensor_scalar(out, in0, s1, s2, o0, o1))

    def tt(deps, out, a, b, o):
        return op("v", deps, lambda e: e.tensor_tensor(out, a, b, o))

    def cp(deps, out, a):
        return op("v", deps, lambda e: e.tensor_copy(out, a))

    def fill(deps, out, c):
        return op("v", deps, lambda e: e.memset(out, c))

    def act(deps, out, a, f=None, **kw):
        f = f or (AF.Identity if kw else AF.Copy)
        return op("a", deps, lambda e: e.activation(out, a, f, **kw))

    def mm(deps, out, lhsT, rhs, start, stop, mark=None):
        return op("t", deps, lambda e: e.matmul(out, lhsT, rhs, start, stop), stop if mark is None else mark)

    def iota(deps, out, pattern, base, cm, small=False):
        if small:
            return op("g", deps, lambda e: e.iota(out, pattern, base, cm, allow_small_or_imprecise_dtypes=True))
        return op("g", deps, lambda e: e.iota(out, pattern, base, cm))

    def mark(deps, out, in_, pattern, base, value):
        return op("g", deps, lambda e: e.affine_select(out, in_, pattern, OP.not_equal, value, base, 1))

    def cols(i, w, at=0):
        return slice(at + w * i, at + w * i + w)

    def send(deps, items):
        wait("g", deps)
        trs = []
        for c, engs, s, srcs, dst in items:
            rid, pid, _ = topo.addr(c)
            trs.append(RemoteDMATransfer(dst_ids=[DstId(rid=rid, pnc=pid)], dma_engine_mask=bits(engs), remote_sem=T.sem[s],
                                         srcs=srcs, dsts=[dst], alu_op=1 if len(srcs) > 1 else 0))
            count["sent"] = count.get("sent", 0) + len(engs)
        g.remote_dma_fused(trs, local_sem=T.sem["sent"])

    far = topo.engines(core, T.cores[ask[0]])
    near = [e for e in topo.engines(core, T.cores[ask[6]]) if e not in far]
    hf = len(far) // 2
    P = [T["p%d" % b] for b in range(8)]

    ent = dma("d_ent", [], T.ent_s[:], T.ent[:])
    zf = fill([], T.zf[:], 0.0)
    zb = fill([], T.zb[:], 0.0)
    zh = fill([], T.zh[:], 0.0)
    one = fill([], T.one[:], 1.0)
    dl = dma("d_dl", [], T.dl[:], T.dic[:])
    waz = dma("d_wa", [zf], T.wa[0:128:16, SP:SP + N * CAP], T.zf[:])
    wvz = dma("d_wv", [zf], T.wv[0:128:16, SP:SP + N * CAP], T.zf[:])
    dma("d_z", [zb], T.fo[:], T.zb[:, 0:144])
    rb = dma("d_z", [], T.rb[:], T.zb[:, 0:144])
    dc = dma("d_dc", [dl], T.dc[:], T.dl[:, :, 16:16 + PL])
    for a in range(3):
        geo = dma("d_geo", [], T.gi[:, cols(a, 256)], T.geo[a:24:3, :])
    for row, src in ((0, T.opa[:]), (14, T.opa[:]), (4, T.hue[0:24:3, :]), (8, T.hue[1:24:3, :]), (12, T.hue[2:24:3, :])):
        dma("d_att", [], T.aw[row:128:16, :], src)
    for a in range(4):
        dma("d_att", [], T.aw[32 * a + 1:32 * a + 32:2, :], T.dic[:])
    for k in range(8):
        dic = dma("d_dic", [dc], T.dw[cols(k, 16), :], T.dc[:])

    i3 = iota([], T.i3[:], [[-16, 8], [0, 16]], 0, 1)
    tcon = iota([], T.tcon[0:1, :], [[1, 16], [0, 32]], 0, 0, True)
    sh = mark([zh], T.sh[:], T.zh[:], [[-1, 144]], 0, 32.0)
    x3 = ts([i3], T.i3s[:], T.i3[:], 4, OP.arith_shift_right)
    nbd = ts([x3], T.nbd[:], T.i3s[:], 0.0, OP.is_equal, -1.0, OP.mult)
    bd = ts([x3], T.bd[:], T.i3s[:], 0.0, OP.is_equal)
    rs = fill([], T.rs[:], 1024.0)
    l0 = op("g", [nbd], lambda e: e.affine_select(T.l0[:], T.nbd[:], [[-1, 128]], OP.is_gt, 0.0, 0, 1))
    l1 = mark([l0], T.l1[:], T.l0[:], [[-1, 128]], 0, BIG)
    rs = iota([rs], T.rs[:, 0:1024:128], [[-20, 8]], 60, 0, True)
    d0 = act([zb], T.d0[:], T.zb[:], AF.Silu, bias=2 * BIG, scale=0.0)
    d0 = iota([d0], T.d0[:, 0:512:8], [[-16, 64]], DUMP + 16 * 63, 1, True)

    def place(r):
        return orders(T, topo, r)[0].index(rank)

    def d_item(i):
        return (helpers(T, topo, serve[i])[place(serve[i])], dictionary_engines(T, topo, rank)[i], "dh", [T.dc[:]], T.dh[:])


    si = ts([ent], T.si[:], T.ent_s[:], S - 1, OP.bitwise_and)
    ob = ts([ent], T.ob[:], T.ent_s[:], 2.0 ** -12, OP.mult, 135.5 + 2.0 ** -13, OP.add)
    s16 = ts([si], T.s16[:], T.si[:], float(S // 2), OP.subtract)
    mks = [ts([ob], T.mk[:, cols(j, 128)], T.ob[:], 136.0 + ask[N - 1 - j], OP.is_equal) for j in range(N)]
    scs = [op("v", [mks[4 * h + 3], rs], lambda e, h=h: e.tensor_tensor_scan(
        T.sc[:, cols(h, 512)], T.rs[:, cols(h, 512)], T.mk[:, cols(h, 512)], 1024.0, OP.min, OP.add)) for h in range(2)]

    for h in range(2):
        mm([zb, one], P[4 + h][:], T.one[0:1, :], T.zb[0:1, :], True, False)
    for b in range(4):
        mm([tcon], P[b][:], T.one[0:1, :], T.tcon[0:1, :], True, False)
    vv, cnt, slot = [None] * 4, [None] * 2, [None] * 2

    def unwrap(b):
        h, odd = b // 2, b % 2
        for j in range(8):
            p = 2 * j + odd
            t = mm([sh, s16], P[b][:, j:512:8], T.sh[:, p:p + 128], T.s16[:, cols(h, 64)], False, j == 7)
        vv[b] = act([t], T.vv[:, 1024 * h + odd:1024 * h + 1024:2], P[b][:], bias=16.0 * S + 12.5 + 16 * h)

    def later(h):
        for j in range(N):
            mm([mks[j], l1], P[4 + h][:, j:512:8], T.l1[:], T.mk[:, cols(h, 64, 128 * j)], False, False)

    def through(h):
        for j in range(N):
            cnt[h] = mm([scs[j // 4], bd], P[4 + h][:, j:512:8], T.bd[:], T.sc[:, cols(h, 64, 128 * j)], False, j == N - 1)

    unwrap(0)
    unwrap(1)
    unwrap(2)
    later(0)
    through(0)
    unwrap(3)
    later(1)
    through(1)
    for h in range(2):
        ms = op("v", [cnt[h], d0], lambda e, h=h: e.tensor_tensor_scan(
            T.ms[:, cols(h, 512)], T.d0[:], P[4 + h][:], 65536.0, OP.min, OP.max))
        slot[h] = ts([ms], T.slot[:, cols(h, 64)], T.ms[:, 512 * h + 7:512 * h + 512:8], float(DUMP), OP.subtract)
    sa = act([slot[0], vv[1], waz], T.wa[:].indirect(T.slot[:, 0:64]), T.vv[:, 0:1024], AF.Silu)
    sa = act([slot[1], sa], T.wa[:].indirect(T.slot[:, 64:CUT]), T.vv[:, 1024:16 * CUT], AF.Silu)
    sv = cp([slot[1], vv[3], wvz], T.wv[:].indirect(T.slot[:, CUT:128]), T.vv[:, 16 * CUT:NE])

    lq = [None] * 4
    for q, win, dep, to in (("a", T.wa, sa, T.ra), ("s", T.wv, sv, T.rv)):
        for i in range(N - 1):
            k = min(i // 2, 2)
            lq[k] = dma("lq%d" % k, [dep], to[i], win[0:128:16, cols(i, CAP, SP)], q)
    gb = cp([geo], T.gb[:], T.gi[:])
    for a, q in enumerate("sas"):
        att = dma("d_att", [gb], T.aw[2 + 4 * a:128:16, :], T.gb[:, cols(a, 256)], q)
    for q, win, to in (("a", T.wa, T.rqa), ("s", T.wv, T.rqv)):
        lq[3] = dma("lq3", [], to[:], win[0:128:16, cols(N - 1, CAP, SP)], q)

    for row, weight in ((2, float(PL)), (6, -1.0), (10, -16.0)):
        rb = mark([rb], T.rb[:, 16:144:16], T.rb[:, 16:144:16], [[-16, 8]], -row, weight)
    fo = mark([], T.fo[:, 3:131:4], T.fo[:, 3:131:4], [[-16, 8], [-4, 4]], 0, 1.0)
    send([dc], [d_item(i) for i in range(SH)])
    act([sh], T.sb[:], T.sh[:], scale=2.0 ** -5)
    sb = idf = act([], T.idf[:], T.sh[:, 0:128], scale=2.0 ** -5)
    iota([], T.kc[0:1, 0:128], [[6, 8], [48, 8], [1, 2]], 0, 0, True)
    kc = act([], T.kc[0:1, 128:256], T.one[0:1, :])
    ip = iota([], T.ip[0:1, 0:6], [[2, 3], [384, 2]], 0, 0, True)
    bo = mark([], T.bo[:], T.zb[:], [[-1, 4], [-16, 8], [0, 16]], 0, 1.0)

    def rq_item(i, engs):
        at = orders(T, topo, ask[i])[1].index(rank)
        return (T.cores[ask[i]], engs, "rq%d" % (at // 2), [T.ra[i], T.rv[i]], T.rqi[:, cols(at, LW)])

    send([lq[0]], [rq_item(0, far[:hf]), rq_item(1, far[hf:])])
    send([lq[1]], [rq_item(2, far[:hf]), rq_item(3, far[hf:])])
    send([lq[2]], [rq_item(4, far[:hf]), rq_item(5, far[hf:])])
    send([], [rq_item(6, near)])
    selc = mark([], T.selc[:], T.zb[:, 0:24], [[-16, 8], [-4, 3]], -4, 1.0)
    rq_in = [("rq0", 2 * hf), ("rq1", 2 * hf), ("rq2", 2 * hf), ("rq3", len(near))]


    at0 = float(DUMP + SP)
    m7 = T.ms[:, 7:1024:8]
    xd = ts([], T.xd[:], m7, at0 + 9.5, OP.subtract, 0.05, OP.mult)
    xa = act([ms], T.xa[:], m7, scale=16.0, bias=Z - 16 * at0)
    xp = ts([xd], T.xp[:], T.xd[:], 4, OP.arith_shift_right)
    xb = ts([xd], T.xb[:], T.xd[:], -319.0, OP.mult)
    xc = ts([xp], T.xc[:], T.xp[:], 304.0, OP.mult)
    for n, x in enumerate((T.xa, T.xb, T.xc)):
        t = mm([xa, xc, idf, vv[3]], P[0][:, 0:128], T.idf[:], x[:], n == 0, n == 2)
    mm([kc, ip], P[1][:, 0:6], T.kc[0:1, 0:128], T.kc[0:1, 128:134], True, False)
    pick = mm([], P[1][:, 0:6], T.kc[0:1, 128:256], T.ip[0:1, 0:6], False, True)
    fin = t
    st = act([], T.st[:], T.zb[:])
    gwz = act([], T.gw[:, 0:Z], T.zb[:, 0:Z])
    alz = act([], T.al[:, 0:Z], T.zb[:, 0:Z])
    omz = act([], T.om[:, 0:1], T.one[:, 0:1])
    st = act([st], T.st[:, 0:512:64], T.one[:, 0:8])
    rqo = tt([lq[3]], T.rqi[:, cols(N - 1, LW)], T.rqa[:], T.rqv[:], OP.add)
    half = mark([], T.half[:], T.zf[:, 0:2], [[0, 2]], 1, 0.0)
    half = op("g", [half], lambda e: e.affine_select(T.half[:, 0:1], T.half[:, 0:1], [[0, 1]], OP.is_ge, 1.0, -64, 1))
    half = op("g", [half], lambda e: e.affine_select(T.half[:, 1:2], T.half[:, 1:2], [[0, 1]], OP.is_gt, 1.0, 64, -1))

    su, of, col, base, fold, fe = ([None] * N for _ in range(6))
    ga, ft = [[] for _ in range(N)], [[] for _ in range(N)]
    lot, folds_lot = [], []

    def mark_all(x, a, b, t):
        for i in range(a, b):
            x[i] = t

    def splats(a, b):
        c = slice(LW * a, LW * b)
        magic = 1.5 * 2.0 ** 26
        x = ts([rq_in[i // 2] if i < N - 1 else rqo for i in range(a, b)], T.su[:, c], T.rqi[:, c], 28.0, OP.subtract,
               2.0 ** -5, OP.mult)
        mark_all(su, a, b, x)
        ts([], T.r8[:, c], T.rqi[:, c], magic, OP.add, magic, OP.subtract)
        mark_all(of, a, b, ts([x], T.s64[:, c], T.su[:, c], -64.0, OP.mult, 120 - 28.5, OP.add))

    def rows(x, y, step=1):
        return T.gq[:, x:y:step] if x < CAP * (N - 1) else T.gw[:, Z + x:Z + y:step]

    def attr(a, b, by_vector):
        m = LW * a + by_vector
        for by, x, y in ((cp, LW * a, m), (act, m, LW * b)):
            if y > x:
                t = by(su[a:b] + [att], rows(16 * x, 16 * y), T.aw[:].indirect(T.su[:, x:y]))
                for i in range(a, b):
                    ga[i].append(t)

    def tiles(a, b):
        k = len(lot)
        lot.append((a, b))
        for n, x in enumerate((T.s64, T.rqi, T.r8)):
            mm(of[a:b] + [idf] + (col[slice(*lot[k - 2])] if k > 1 else []), P[6 + k % 2][:, 0:LW * (b - a)], T.idf[:],
               x[:, LW * a:LW * b], n == 0, False)

    def lists(a, b):
        for p in range(16):
            base[a] = mm(sum(ga[a:b], []) + [rb], P[6 + lot.index((a, b)) % 2][:, 0:LW * (b - a)], T.rb[:, 16 - p:144 - p],
                         rows(CAP * a + p, CAP * b, 16), False, p == 15)

    def folds(a, b):
        k = len(folds_lot)
        folds_lot.append((a, b))
        lot = folds_lot
        for i in range(a, b):
            for h in range(4):
                fold[a] = mm(ga[i] + [fo, ms, fe[lot[k - 2][0]] if k > 1 else None], P[4 + k % 2][:, cols(i - a, FW)],
                             T.fo[:, 3 - h:131 - h], T.gq[:, cols(h, FW, CAP * i)], h == 0, h == 3, h == 3 and i == b - 1)

    def columns(a, b):
        k = [x <= a < y for x, y in lot].index(True)
        first = lot[k][0]
        o = P[6 + k % 2][:, LW * (a - first):LW * (b - first)]
        if a >= SH:
            return mark_all(col, a, b, cp([base[first]], T.cu[:, LW * a:LW * b], o))
        magic = 1.5 * 2.0 ** 28
        hi = ts([base[first]], T.fs[:, a:b, FW:FW + LW], o, magic, OP.add, magic, OP.subtract)
        mark_all(col, a, b, tt([hi], T.fs[:, a:b, FW + LW:SW], o, T.fs[:, a:b, FW:FW + LW], OP.subtract))

    def folded(a, b):
        out = T.fs[:, a:b, 0:FW] if a < SH else T.fq[:, a:b, CAP:RW]
        mark_all(fe, a, b, act([fold[a]], out, P[4 + folds_lot.index((a, b)) % 2][:, 0:FW * (b - a)]))

    def foot(i, by_vector=LW // 2):
        for by, a, b in ((cp, 0, by_vector), (act, by_vector, LW)):
            if b > a and i >= SH:
                ft[i].append(by([col[i], dic], T.fq[:, i, 16 * a:16 * b], T.dw[:].indirect(T.cu[:, LW * i + a:LW * i + b])))
            elif b > a:
                ft[i].append(by([cx[i], ("xw%d" % i, len(far + near))], T.fw[:, i, 16 * a:16 * b],
                                T.xw[:, cols(i, DW)].indirect(T.cx[:, LW * i + a:LW * i + b])))

    def answer(*items):
        out = []
        for i, engs in items:
            at = place(serve[i])
            src, dst = (T.fs[:, i, :], T.fx[:, at, :]) if i < SH else (T.fq[:, i, :], T.fw[:, at, :])
            out.append((T.cores[serve[i]], engs, "f%d" % at, [src], dst))
        send([t for i, _ in items for t in ft[i] + [fe[i], col[i]]], out)

    def answer_neighbour(footprints):
        i = N - 2
        if footprints:
            return send(ft[i], [(T.cores[serve[i]], near, "f7", [T.fq[:, i, 0:CAP]], T.fw[:, i, 0:CAP])])
        send(ga[i], [(T.cores[serve[i]], near, "f6", [rows(CAP * i, CAP * i + CAP)], T.gw[:, cols(i, CAP, Z)])])

    landed = [("f%d" % i, len(far) // LANES[i]) for i in range(N - 2)] + [("f6", len(near))]
    al, un, und, theirs, cx = [], [], [], [], [None] * SH

    def folded_of(i):
        if i >= N - 2:
            return T.gw[:, cols(i, CAP, Z)], ga[i] if i == N - 1 else [landed[i]]
        return T.fx[:, i, 0:FW] if i < SH else T.fw[:, i, CAP:RW], [landed[i]]

    def alpha(i):
        f, d = folded_of(i)
        n = len(al)
        parts, w = (4, FW) if i < N - 2 else (1, CAP)
        for h in range(parts):
            a = mm(d + [bo, pick, al[n - 2] if n > 1 else None], P[n % 2][:, cols(h, w)], T.bo[:, cols(h, 128)], f,
                   True, True, h == parts - 1)
        mine = ft[i] if i < SH or i == N - 1 else [("f7", len(near))] if i == N - 2 else [landed[i]]
        al.append(tt(d + mine + [a], T.al[:, cols(i, CAP, Z)], P[n % 2][:, 0:CAP],
                     T.fq[:, i, 0:CAP] if i == N - 1 else T.fw[:, i, 0:CAP], OP.mult))

    def hues(i, by=act):
        f, d = folded_of(i)
        m = len(un)
        for h in range(4):
            u = mm(d + [vv[3], un[m - 2] if m > 1 else None], P[2 + m % 2][:, cols(h, FW)], T.sb[:, h:h + 128], f,
                   True, True, h == 3)
        un.append(by([u], T.gw[:, cols(i, CAP, Z)], P[2 + m % 2][:, 0:CAP]))

    def their_columns(a, b):
        o = P[6 + len(lot) % 2]
        for i in range(a, b):
            mm([landed[i], sb] + col, o[:, cols(i, LW)], T.sb[:, 0:128], T.fx[:, i, FW:FW + LW], True, False)
            t = mm([], o[:, cols(i, LW)], T.sb[:, 0:128], T.fx[:, i, FW + LW:SW], False, True)
        theirs.append(cp([t], T.cx[:, LW * a:LW * b], o[:, LW * a:LW * b]))
        mark_all(cx, a, b, theirs[-1])

    splats(7, 8)
    attr(7, 8, 0)
    fin = cp([fin], T.fin[:], P[0][:, 0:128])
    pick = cp([pick], T.pick[:, 0:6], P[1][:, 0:6])
    tiles(7, 8)
    lists(7, 8)
    splats(0, 2)
    attr(0, 2, 16)
    splats(2, 4)
    attr(2, 4, 8)
    tiles(0, 2)
    lists(0, 2)
    folds(0, 2)
    columns(7, 8)
    columns(0, 2)
    folded(0, 2)
    answer((0, far[:hf]), (1, far[hf:]))
    tiles(2, 4)
    splats(4, 7)
    lists(2, 4)
    attr(4, 7, 22)
    answer_neighbour(False)
    folds(2, 4)
    tiles(4, 7)
    columns(2, 4)
    lists(4, 7)
    foot(2, 18)
    folded(2, 4)
    answer((2, far))
    foot(3, 2)
    answer((3, far))
    folds(4, 6)
    columns(4, 7)
    folded(4, 6)
    foot(4, LW)
    answer((4, far))
    foot(6, 0)
    answer_neighbour(True)
    foot(5, 16)
    answer((5, far))

    foot(7, 12)
    hues(1)
    their_columns(0, 2)
    alpha(7)
    foot(0, 4)
    alpha(0)
    alpha(2)
    foot(1, 0)
    hues(0)
    alpha(1)
    hues(2)
    alpha(3)
    hues(3)
    alpha(6)
    hues(4)
    alpha(4)
    hues(5)
    alpha(5)

    plan = {q: [(w[0], int(w[1], 17), int(w[2], 17)) for w in PLAN[q].split()] for q in PLAN}
    done = {s: [None] * 16 for s in "RLWTKGCXMO"}
    ready = [al[-1], alz, fin]
    lots = {s: sorted((a, b) for q in "va" for r, a, b in plan[q] if r == s) for s in "KXO"}
    banks = {"K": (0, 1, 6, 7), "X": (4, 5), "O": (2, 3)}

    def bank(s, x):
        n = [a <= x < b for a, b in lots[s]].index(True)
        m = len(banks[s])
        return P[banks[s][n % m]], x - lots[s][n][0], range(*lots[s][n - m]) if n >= m else ()

    def needs(s, a, b):
        blocks = range(a, b)
        out = [(r, x) for r in {"L": "R", "W": "L", "T": "W", "K": "T", "C": "G", "X": "C", "M": "KX", "O": "M"}.get(s, "")
               for x in blocks]
        to = {"T": "K", "C": "X", "M": "O"}.get(s)
        if to:
            out += [(to, y) for x in blocks for y in bank(to, x)[2]]
        return out + ([("R", a - 1)] if s == "L" and a else [])

    def step(q, s, a, b):
        d = [done[r][x] for r, x in needs(s, a, b)]
        by = cp if q == "v" else act
        e, f = slice(128 * a, 128 * b), T.fin[:, 8 * a:8 * b]
        if s == "R":
            t = act(ready + [omz], T.om[:, 128 * a + 1:128 * b + 1], T.al[:].indirect(f), scale=-1.0, bias=1.0)
        elif s == "L":
            t = op("v", d + [st], lambda v: v.tensor_tensor_scan(T.li[:, e], T.om[:, e], T.st[:, 0:128 * (b - a)], 1.0,
                                                                OP.mult, OP.max))
        elif s == "W":
            t = tt(d + ready, T.ww[:, e], T.al[:].indirect(f), T.li[:, e], OP.mult)
        elif s == "G":
            t = by(un + ga[N - 1] + [landed[N - 2], gwz, fin], T.ge[:, e], T.gw[:].indirect(f))
        elif s == "K":
            t = by(d, T.wt[:, e], bank(s, a)[0][:, 0:128 * (b - a)])
        elif s == "X":
            for h in range(2):
                o, x, m = T.ct[:, 48 * a + h:48 * b:2], bank(s, a)[0][:, 0:24 * (b - a)], T.half[:, h:h + 1]
                t = ts(d + [half], o, x, m, OP.mult) if q == "v" else act(d + [half], o, x, scale=m)
        elif s == "O":
            t = by(d, T.ya[:, 48 * a:48 * b], bank(s, a)[0][:, 0:48 * (b - a)])
        else:
            for x in range(a, b):
                o, at, _ = bank({"T": "K", "C": "X", "M": "O"}[s], x)
                if s == "T":
                    t = op("t", d + [idf] + theirs, lambda p, o=o, at=at, x=x: p.transpose(
                        o[:, cols(at, 128)], T.ww[:, cols(x, 128)], T.idf[:]), x == b - 1)
                elif s == "C":
                    t = mm(d + [selc] + fe, o[:, cols(at, 24)], T.ge[:, cols(x, 128)], T.selc[:], True, True, x == b - 1)
                else:
                    t = mm(d + un, o[:, cols(at, 48)], T.wt[:, cols(x, 128)], T.ct[:, cols(x, 48)], True, True, x == b - 1)
        for x in range(a, b):
            done[s][x] = t

    while any(plan.values()):
        q = [q for q in "vat" if plan[q] and all(done[r][x] for r, x in needs(*plan[q][0]))][0]
        step(q, *plan[q].pop(0))
    yo = cp(done["O"] + [pick], T.yo[:], T.ya[:].indirect(T.pick[:, 0:6]))
    y = dma("d_y", [yo], T.y[:], T.yo[:])

    wait("s", [y])
    wait("g", [(s, count[s]) for s in ("cv", "ca", "ct", "cg", "sent")])
